import numpy as np
import ml_dtypes


def mxq(x, axis, fmt="e4m3"):
    dtype, down = {"e4m3": (ml_dtypes.float8_e4m3fn, 7), "e5m2": (ml_dtypes.float8_e5m2, 14)}[fmt]
    v = np.moveaxis(np.asarray(x, np.float32).astype(ml_dtypes.bfloat16).astype(np.float64), axis, -1)
    blocks = v.reshape(v.shape[:-1] + (-1, 32))
    amax = np.abs(blocks).max(-1, keepdims=True)
    byte = np.maximum(np.where(amax > 0, np.frexp(amax)[1] - 1 + 127, 0) - down, 1)
    scale = np.exp2(byte - 127.0)
    codes = (blocks / scale).astype(np.float32).astype(dtype).astype(np.float64)
    return np.moveaxis((codes * scale).reshape(v.shape), -1, axis)


WIDE = False


def mx_kscale(k):
    if not WIDE:
        return np.ones(k)
    levels = np.array([10, -10, 5, -5, 0])
    if k % 512:
        return np.exp2(np.random.permutation(np.resize(levels, k // 32))).repeat(32)
    a = np.empty((k // 512, 16))
    for p in range(k // 512):
        a[p, :8] = np.random.permutation(np.resize(levels, 8))
        for g in range(8):
            far = levels[np.abs(levels - a[p, g]) >= 10]
            a[p, g + 8] = far[np.random.randint(len(far))]
    return np.exp2(a.ravel()).repeat(32)


def f64(x):
    return np.asarray(x).astype(np.float64)


def striped(idx):
    return np.tile(idx.reshape(-1, 16).T, (8, 1)).astype(np.uint16)


def unstriped(offs):
    return offs[:16].T.reshape(-1).astype(np.int64)


def striped8(idx):
    return np.concatenate([x.reshape(-1, 16).T for x in idx]).astype(np.uint16)


def runs(offs, k):
    lists = np.stack([offs[16 * r : 16 * r + 16].T.reshape(-1) for r in range(8)]).astype(np.int64)
    return lists[np.arange(k) % 512 // 64]


def pack_weight(w):
    k, n = w.shape
    w = f64(np.asarray(w, np.float32).astype(ml_dtypes.bfloat16)).reshape(k // 32, 32, n)
    amax = np.abs(w).max(1)
    byte = np.clip(np.where(amax > 0, np.frexp(amax)[1] - 1 + 127 - 7, 1), 1, 254)
    scaled = (w * np.exp2(127.0 - byte)[:, None, :]).reshape(k, n).astype(np.float32)
    words = np.ascontiguousarray(scaled.reshape(k // 512, 128, 4, n).transpose(0, 1, 3, 2)).astype(ml_dtypes.float8_e4m3fn).view(np.uint8)
    return words, np.ascontiguousarray(byte.astype(np.uint8).reshape(k // 512, 16, n))


def unpack_weight(words, scales):
    g, p, n, _ = words.shape
    vals = np.ascontiguousarray(words).view(ml_dtypes.float8_e4m3fn).astype(np.float64) * np.repeat(np.exp2(scales.astype(np.float64) - 127.0), 8, axis=1)[..., None]
    return vals.transpose(0, 1, 3, 2).reshape(g * 512, n)


K, T, S, N, U = 1024, 2048, 512, 512, 512


def setup_inputs():
    n = np.random.standard_normal
    s = mx_kscale(K)[:, None]
    packed_xT = pack_weight(n((K, T)) * s)
    return {
        "x_words": packed_xT[0],
        "x_scales": packed_xT[1],
        "w1": (n((K, N)) / np.sqrt(K) / s).astype(np.float32),
        "cs": np.repeat(np.random.uniform(0.5, 4.0, (8, U)), 64, axis=0).astype(np.float32),
        "offs": striped(np.random.permutation(T)[:S]),
        "col": striped8(np.random.randint(0, U, (8, S))),
    }


def reference(x_words, x_scales, w1, cs, offs, col):
    xq = unpack_weight(x_words, x_scales)[:, unstriped(offs)]
    y = mxq(f64(w1), 0, "e4m3").T @ xq
    e = np.exp(y - y.max(axis=1, keepdims=True))
    sm = e / e.sum(axis=1, keepdims=True)
    return sm * (f64(cs)[np.arange(N)[:, None], runs(col, N)])

@@ -1,0 +1,110 @@
+from contextlib import ExitStack
+
+import concourse.mybir as mybir
+
+K, T, S, N, U = 1024, 2048, 512, 512, 512
+FLOPS = 2 * K * N * S
+
+F32 = mybir.dt.float32
+BF16 = mybir.dt.bfloat16
+I32 = mybir.dt.int32
+U32 = mybir.dt.uint32
+U16 = mybir.dt.uint16
+U8 = mybir.dt.uint8
+FP8X4 = mybir.dt.float8_e4m3fn_x4
+ALU = mybir.AluOpType
+ACT = mybir.ActivationFunctionType
+AX = mybir.AxisListType
+
+P = 128
+PACK = 4
+K_PASS = P * PACK
+PASSES = K // K_PASS
+TILES = N // P
+
+
+def tile_picked_sinkcol_none_p_kernel(tc, x_words, x_scales, w1, cs, offs, col, out):
+    nc = tc.nc
+    with ExitStack() as ctx:
+        lists = ctx.enter_context(tc.tile_pool(name="lists", bufs=1))
+        sb = ctx.enter_context(tc.tile_pool(name="sb", bufs=1))
+        psum = ctx.enter_context(tc.psum_pool(name="psum", bufs=1))
+
+        offs_sb = lists.tile([P, S // 16], U16, name="offs_sb")
+        col_sb = lists.tile([P, S // 16], U16, name="col_sb")
+
+        scale_table = sb.tile([P, T], U8, name="scale_table", align_bytes=64)
+        nc.vector.memset(scale_table[:].bitcast(I32), 0)
+
+        w_raw = [sb.tile([P, PACK, N], F32, name=f"w_raw{z}", align_bytes=64) for z in range(PASSES)]
+        word_table = [sb.tile([P, T], I32, name=f"word_table{z}", align_bytes=64) for z in range(PASSES)]
+        cs_table = sb.tile([P, U], F32, name="cs_table", align_bytes=64)
+
+        nc.sync.dma_start(out=w_raw[0][:], in_=w1[0:K_PASS, :].rearrange("(p j) n -> p j n", j=PACK))
+        nc.sync.dma_start(offs_sb[:], offs)
+        nc.sync.dma_start(col_sb[:], col)
+        nc.sync.dma_start(out=cs_table[:], in_=cs.rearrange("(p t) u -> p t u", t=TILES)[:, 0, :])
+        for q in range(4):
+            nc.scalar.dma_start(
+                out=scale_table[32 * q : 32 * q + 4 * PASSES, :].bitcast(I32),
+                in_=x_scales[:, 4 * q : 4 * q + 4, :].bitcast(I32),
+            )
+        nc.sync.dma_start(out=w_raw[1][:], in_=w1[K_PASS : 2 * K_PASS, :].rearrange("(p j) n -> p j n", j=PACK))
+        for z in range(PASSES):
+            nc.sync.dma_start(out=word_table[z][:], in_=x_words[z].rearrange("p c r -> p (c r)").bitcast(I32))
+
+        cs_picked = sb.tile([P, S], F32, name="cs_picked", align_bytes=64)
+        half = S // 2
+        for h in range(2):
+            nc.vector.tensor_copy(
+                cs_picked[:, h * half : (h + 1) * half],
+                cs_table[:].indirect(col_sb[:, h * half // 16 : (h + 1) * half // 16]),
+            )
+        x_planes = sb.tile([P, S], U8, name="x_planes", align_bytes=64)
+        nc.vector.tensor_copy(x_planes[:], scale_table[:].indirect(offs_sb[:]))
+
+        w_codes, w_planes, x_codes = [], [], []
+        for z in range(PASSES):
+            grouped = sb.tile([P, N * PACK], BF16, name=f"grouped{z}", align_bytes=64)
+            nc.scalar.copy(
+                out=grouped[:].rearrange("p (t c j) -> p c j t", t=TILES, j=PACK),
+                in_=w_raw[z][:].rearrange("p j (c t) -> p c j t", t=TILES),
+            )
+            codes = sb.tile([P, N], U32, name=f"w_codes{z}", align_bytes=64)
+            plane = sb.tile([P, N], U8, name=f"w_plane{z}", align_bytes=64)
+            nc.vector.quantize_mx(out=codes[:].bitcast(FP8X4), scales=plane[:], in_=grouped[:])
+            w_codes.append(codes)
+            w_planes.append(plane)
+        for z in range(PASSES):
+            picked = sb.tile([P, S], U32, name=f"x_codes{z}", align_bytes=64)
+            nc.vector.tensor_copy(picked[:], word_table[z][:].bitcast(U32).indirect(offs_sb[:]))
+            x_codes.append(picked)
+
+        scores = [psum.tile([P, S], F32, name=f"scores{t}") for t in range(TILES)]
+        for z in range(PASSES):
+            for t in range(TILES):
+                cols = slice(t * P, (t + 1) * P)
+                nc.tensor.matmul_mx(
+                    out=scores[t][:],
+                    lhsT=w_codes[z][:, cols].bitcast(FP8X4),
+                    lhsT_scale=w_planes[z][:, cols],
+                    rhs=x_codes[z][:].bitcast(FP8X4),
+                    rhs_scale=x_planes[4 * z : P, :],
+                    start=(z == 0),
+                    stop=(z == PASSES - 1),
+                )
+
+        out_rows = out.rearrange("(p t) s -> p t s", t=TILES)
+        for t in range(TILES):
+            neg_max = sb.tile([P, 1], F32, name=f"neg_max{t}")
+            nc.vector.tensor_reduce(out=neg_max[:], in_=scores[t][:], axis=AX.X, op=ALU.max, negate=True)
+            expd = sb.tile([P, S], F32, name=f"expd{t}")
+            total = sb.tile([P, 1], F32, name=f"total{t}")
+            nc.scalar.activation(out=expd[:], in_=scores[t][:], func=ACT.Exp, bias=neg_max[:], scale=1.0, accum_out=total[:])
+            inv = sb.tile([P, 1], F32, name=f"inv{t}")
+            nc.vector.reciprocal(out=inv[:], in_=total[:])
+            result = sb.tile([P, S], F32, name=f"result{t}")
+            nc.vector.scalar_tensor_tensor(
+                out=result[:], in0=expd[:], scalar=inv[:], in1=cs_picked[:], op0=ALU.mult, op1=ALU.mult
+            )
+            nc.sync.dma_start(out=out_rows[:, t, :], in_=result[:])

@@ -38,14 +38,14 @@ def tile_picked_sinkcol_none_p_kernel(tc, x_words, x_scales, w1, cs, offs, col, 
 
         w_raw = [sb.tile([P, PACK, N], F32, name=f"w_raw{z}", align_bytes=64) for z in range(PASSES)]
         word_table = [sb.tile([P, T], I32, name=f"word_table{z}", align_bytes=64) for z in range(PASSES)]
-        cs_table = sb.tile([P, U], F32, name="cs_table", align_bytes=64)
+        cs_table = sb.tile([P, U], F32, name="cs_table", tag="cs_table", align_bytes=64)
 
-        nc.sync.dma_start(out=w_raw[0][:], in_=w1[0:K_PASS, :].rearrange("(p j) n -> p j n", j=PACK))
-        nc.sync.dma_start(offs_sb[:], offs)
         nc.sync.dma_start(col_sb[:], col)
+        nc.sync.dma_start(offs_sb[:], offs)
         nc.sync.dma_start(out=cs_table[:], in_=cs.rearrange("(p t) u -> p t u", t=TILES)[:, 0, :])
+        nc.sync.dma_start(out=w_raw[0][:], in_=w1[0:K_PASS, :].rearrange("(p j) n -> p j n", j=PACK))
         for q in range(4):
-            nc.scalar.dma_start(
+            nc.gpsimd.dma_start(
                 out=scale_table[32 * q : 32 * q + 4 * PASSES, :].bitcast(I32),
                 in_=x_scales[:, 4 * q : 4 * q + 4, :].bitcast(I32),
             )
@@ -60,16 +60,19 @@ def tile_picked_sinkcol_none_p_kernel(tc, x_words, x_scales, w1, cs, offs, col, 
                 cs_picked[:, h * half : (h + 1) * half],
                 cs_table[:].indirect(col_sb[:, h * half // 16 : (h + 1) * half // 16]),
             )
-        x_planes = sb.tile([P, S], U8, name="x_planes", align_bytes=64)
+        x_planes = sb.tile([P, S], U8, name="x_planes", tag="cs_table", align_bytes=64)
         nc.vector.tensor_copy(x_planes[:], scale_table[:].indirect(offs_sb[:]))
 
         w_codes, w_planes, x_codes = [], [], []
         for z in range(PASSES):
             grouped = sb.tile([P, N * PACK], BF16, name=f"grouped{z}", align_bytes=64)
-            nc.scalar.copy(
-                out=grouped[:].rearrange("p (t c j) -> p c j t", t=TILES, j=PACK),
-                in_=w_raw[z][:].rearrange("p j (c t) -> p c j t", t=TILES),
-            )
+            dst = grouped[:].rearrange("p (t c j) -> p c j t", t=TILES, j=PACK)
+            src = w_raw[z][:].rearrange("p j (c t) -> p c j t", t=TILES)
+            if z == 0:
+                nc.scalar.copy(out=dst, in_=src)
+            else:
+                nc.scalar.copy(out=dst[:, 0 : P // 2], in_=src[:, 0 : P // 2])
+                nc.vector.tensor_copy(out=dst[:, P // 2 : P], in_=src[:, P // 2 : P])
             codes = sb.tile([P, N], U32, name=f"w_codes{z}", align_bytes=64)
             plane = sb.tile([P, N], U8, name=f"w_plane{z}", align_bytes=64)
             nc.vector.quantize_mx(out=codes[:].bitcast(FP8X4), scales=plane[:], in_=grouped[:])
@@ -95,16 +98,23 @@ def tile_picked_sinkcol_none_p_kernel(tc, x_words, x_scales, w1, cs, offs, col, 
                 )
 
         out_rows = out.rearrange("(p t) s -> p t s", t=TILES)
+        totals = sb.tile([P, TILES], F32, name="totals")
+        expd = []
         for t in range(TILES):
             neg_max = sb.tile([P, 1], F32, name=f"neg_max{t}")
             nc.vector.tensor_reduce(out=neg_max[:], in_=scores[t][:], axis=AX.X, op=ALU.max, negate=True)
-            expd = sb.tile([P, S], F32, name=f"expd{t}")
-            total = sb.tile([P, 1], F32, name=f"total{t}")
-            nc.scalar.activation(out=expd[:], in_=scores[t][:], func=ACT.Exp, bias=neg_max[:], scale=1.0, accum_out=total[:])
-            inv = sb.tile([P, 1], F32, name=f"inv{t}")
-            nc.vector.reciprocal(out=inv[:], in_=total[:])
-            result = sb.tile([P, S], F32, name=f"result{t}")
-            nc.vector.scalar_tensor_tensor(
-                out=result[:], in0=expd[:], scalar=inv[:], in1=cs_picked[:], op0=ALU.mult, op1=ALU.mult
+            numer = sb.tile([P, S], F32, name=f"expd{t}", tag=f"expd{t}")
+            nc.scalar.activation(
+                out=numer[:], in_=scores[t][:], func=ACT.Exp, bias=neg_max[:], scale=1.0, accum_out=totals[:, t : t + 1]
             )
-            nc.sync.dma_start(out=out_rows[:, t, :], in_=result[:])
+            expd.append(numer)
+        for pair in range(TILES // 2):
+            inv = sb.tile([P, 2], F32, name=f"inv{pair}", tag="inv0" if pair == 0 else "expd0")
+            nc.vector.reciprocal(out=inv[:], in_=totals[:, 2 * pair : 2 * pair + 2])
+            for i in range(2):
+                t = 2 * pair + i
+                result = sb.tile([P, S], F32, name=f"result{t}")
+                nc.vector.scalar_tensor_tensor(
+                    out=result[:], in0=expd[t][:], scalar=inv[:, i : i + 1], in1=cs_picked[:], op0=ALU.mult, op1=ALU.mult
+                )
+                nc.sync.dma_start(out=out_rows[:, t, :], in_=result[:])

@@ -19,8 +19,9 @@ AX = mybir.AxisListType
 P = 128
 PACK = 4
 K_PASS = P * PACK
-PASSES = K // K_PASS
 TILES = N // P
+STRIPE = 16
+HALF = S // 2
 
 
 def tile_picked_sinkcol_none_p_kernel(tc, x_words, x_scales, w1, cs, offs, col, out):
@@ -30,91 +31,137 @@ def tile_picked_sinkcol_none_p_kernel(tc, x_words, x_scales, w1, cs, offs, col, 
         sb = ctx.enter_context(tc.tile_pool(name="sb", bufs=1))
         psum = ctx.enter_context(tc.psum_pool(name="psum", bufs=1))
 
-        offs_sb = lists.tile([P, S // 16], U16, name="offs_sb")
-        col_sb = lists.tile([P, S // 16], U16, name="col_sb")
+        def tile(shape, dtype, name, slot=None):
+            return sb.tile(shape, dtype, name=name, tag=slot or name, align_bytes=64)
 
-        scale_table = sb.tile([P, T], U8, name="scale_table", align_bytes=64)
-        nc.vector.memset(scale_table[:].bitcast(I32), 0)
+        def entries(list_tile, first, last):
+            return list_tile[:, first // STRIPE : last // STRIPE]
 
-        w_raw = [sb.tile([P, PACK, N], F32, name=f"w_raw{z}", align_bytes=64) for z in range(PASSES)]
-        word_table = [sb.tile([P, T], I32, name=f"word_table{z}", align_bytes=64) for z in range(PASSES)]
-        cs_table = sb.tile([P, U], F32, name="cs_table", tag="cs_table", align_bytes=64)
+        offs_sb = lists.tile([P, S // STRIPE], U16, name="offs_sb")
+        col_sb = lists.tile([P, S // STRIPE], U16, name="col_sb")
+        scale_table = tile([P, T], U8, "scale_table")
+        word_table = [tile([P, T], I32, f"word_table{z}") for z in range(2)]
+        w_raw = [tile([P, PACK, N], F32, f"w_raw{z}") for z in range(2)]
+        cs_table = tile([P, U], F32, "cs_table")
 
-        nc.sync.dma_start(col_sb[:], col)
-        nc.sync.dma_start(offs_sb[:], offs)
-        nc.sync.dma_start(out=cs_table[:], in_=cs.rearrange("(p t) u -> p t u", t=TILES)[:, 0, :])
-        nc.sync.dma_start(out=w_raw[0][:], in_=w1[0:K_PASS, :].rearrange("(p j) n -> p j n", j=PACK))
-        for q in range(4):
-            nc.gpsimd.dma_start(
-                out=scale_table[32 * q : 32 * q + 4 * PASSES, :].bitcast(I32),
-                in_=x_scales[:, 4 * q : 4 * q + 4, :].bitcast(I32),
-            )
-        nc.sync.dma_start(out=w_raw[1][:], in_=w1[K_PASS : 2 * K_PASS, :].rearrange("(p j) n -> p j n", j=PACK))
-        for z in range(PASSES):
+        nc.gpsimd.memset(scale_table[:, 0 : T // 2].bitcast(I32), 0)
+        nc.vector.memset(scale_table[:, T // 2 : T].bitcast(I32), 0)
+
+        def load_w(z):
+            rows = w1[z * K_PASS : (z + 1) * K_PASS, :]
+            nc.sync.dma_start(out=w_raw[z][:], in_=rows.rearrange("(p j) n -> p j n", j=PACK))
+
+        def load_scales(z):
+            for a in range(4):
+                nc.sync.dma_start(
+                    out=scale_table[4 * z + a : P : 32, :].bitcast(I32),
+                    in_=x_scales[z, a:16:4, :].bitcast(I32),
+                )
+
+        def load_words(z):
             nc.sync.dma_start(out=word_table[z][:], in_=x_words[z].rearrange("p c r -> p (c r)").bitcast(I32))
 
-        cs_picked = sb.tile([P, S], F32, name="cs_picked", align_bytes=64)
-        half = S // 2
-        for h in range(2):
+        nc.sync.dma_start(col_sb[:], col)
+        load_w(0)
+        nc.sync.dma_start(offs_sb[:], offs)
+        nc.sync.dma_start(out=cs_table[:], in_=cs.rearrange("(p t) u -> p t u", t=TILES)[:, 0, :])
+        load_scales(0)
+        load_words(0)
+        load_scales(1)
+        load_w(1)
+        load_words(1)
+
+        def interleave(copy, grouped, raw, first, last):
+            dst = grouped[:].rearrange("p (t c j) -> p c j t", t=TILES, j=PACK)
+            src = raw[:].rearrange("p j (c t) -> p c j t", t=TILES)
+            copy(out=dst[:, first:last], in_=src[:, first:last])
+
+        def quantize(grouped, name):
+            codes = tile([P, N], U32, f"{name}_codes")
+            plane = tile([P, N], U8, f"{name}_plane")
+            nc.vector.quantize_mx(out=codes[:].bitcast(FP8X4), scales=plane[:], in_=grouped[:])
+            return codes, plane
+
+        def pick_words(z, picked, first, last):
+            window = word_table[z][:].bitcast(U32)
+            nc.vector.tensor_copy(picked[:, first:last], window.indirect(entries(offs_sb, first, last)))
+
+        cs_picked = tile([P, S], F32, "cs_picked")
+        for first in (0, HALF):
             nc.vector.tensor_copy(
-                cs_picked[:, h * half : (h + 1) * half],
-                cs_table[:].indirect(col_sb[:, h * half // 16 : (h + 1) * half // 16]),
+                cs_picked[:, first : first + HALF], cs_table[:].indirect(entries(col_sb, first, first + HALF))
             )
-        x_planes = sb.tile([P, S], U8, name="x_planes", tag="cs_table", align_bytes=64)
+
+        grouped0 = tile([P, N * PACK], BF16, "grouped0")
+        interleave(nc.scalar.copy, grouped0, w_raw[0], 0, P)
+        w_quant0 = quantize(grouped0, "w0")
+
+        x_planes = tile([P, S], U8, "x_planes", "cs_table")
         nc.vector.tensor_copy(x_planes[:], scale_table[:].indirect(offs_sb[:]))
 
-        w_codes, w_planes, x_codes = [], [], []
-        for z in range(PASSES):
-            grouped = sb.tile([P, N * PACK], BF16, name=f"grouped{z}", align_bytes=64)
-            dst = grouped[:].rearrange("p (t c j) -> p c j t", t=TILES, j=PACK)
-            src = w_raw[z][:].rearrange("p j (c t) -> p c j t", t=TILES)
-            if z == 0:
-                nc.scalar.copy(out=dst, in_=src)
-            else:
-                nc.scalar.copy(out=dst[:, 0 : P // 2], in_=src[:, 0 : P // 2])
-                nc.vector.tensor_copy(out=dst[:, P // 2 : P], in_=src[:, P // 2 : P])
-            codes = sb.tile([P, N], U32, name=f"w_codes{z}", align_bytes=64)
-            plane = sb.tile([P, N], U8, name=f"w_plane{z}", align_bytes=64)
-            nc.vector.quantize_mx(out=codes[:].bitcast(FP8X4), scales=plane[:], in_=grouped[:])
-            w_codes.append(codes)
-            w_planes.append(plane)
-        for z in range(PASSES):
-            picked = sb.tile([P, S], U32, name=f"x_codes{z}", align_bytes=64)
-            nc.vector.tensor_copy(picked[:], word_table[z][:].bitcast(U32).indirect(offs_sb[:]))
-            x_codes.append(picked)
+        x_codes = [tile([P, S], U32, f"x_codes{z}") for z in range(2)]
+        pick_words(0, x_codes[0], 0, S)
+
+        grouped1 = tile([P, N * PACK], BF16, "grouped1", "scale_table")
+        interleave(nc.scalar.copy, grouped1, w_raw[1], 0, P // 2)
+        interleave(nc.vector.tensor_copy, grouped1, w_raw[1], P // 2, P)
+        w_quant1 = quantize(grouped1, "w1")
+        pick_words(1, x_codes[1], 0, HALF)
+        pick_words(1, x_codes[1], HALF, S)
 
         scores = [psum.tile([P, S], F32, name=f"scores{t}") for t in range(TILES)]
-        for z in range(PASSES):
-            for t in range(TILES):
-                cols = slice(t * P, (t + 1) * P)
-                nc.tensor.matmul_mx(
-                    out=scores[t][:],
-                    lhsT=w_codes[z][:, cols].bitcast(FP8X4),
-                    lhsT_scale=w_planes[z][:, cols],
-                    rhs=x_codes[z][:].bitcast(FP8X4),
-                    rhs_scale=x_planes[4 * z : P, :],
-                    start=(z == 0),
-                    stop=(z == PASSES - 1),
-                )
 
-        out_rows = out.rearrange("(p t) s -> p t s", t=TILES)
-        totals = sb.tile([P, TILES], F32, name="totals")
+        def multiply(t, z, w_quant, first, last):
+            codes, plane = w_quant
+            queries = slice(t * P, (t + 1) * P)
+            nc.tensor.matmul_mx(
+                out=scores[t][:, first:last],
+                lhsT=codes[:, queries].bitcast(FP8X4),
+                lhsT_scale=plane[:, queries],
+                rhs=x_codes[z][:, first:last].bitcast(FP8X4),
+                rhs_scale=x_planes[4 * z : P, first:last],
+                start=(z == 0),
+                stop=(z == 1 and last == S),
+            )
+
+        for t in range(TILES):
+            multiply(t, 0, w_quant0, 0, S)
+        for first in (0, HALF):
+            for t in range(TILES // 2):
+                multiply(t, 1, w_quant1, first, first + HALF)
+        for t in range(TILES // 2, TILES):
+            multiply(t, 1, w_quant1, 0, S)
+
+        totals = tile([P, TILES], F32, "totals")
         expd = []
         for t in range(TILES):
-            neg_max = sb.tile([P, 1], F32, name=f"neg_max{t}")
+            neg_max = tile([P, 1], F32, f"neg_max{t}")
             nc.vector.tensor_reduce(out=neg_max[:], in_=scores[t][:], axis=AX.X, op=ALU.max, negate=True)
-            numer = sb.tile([P, S], F32, name=f"expd{t}", tag=f"expd{t}")
+            expd.append(tile([P, S], F32, f"expd{t}"))
             nc.scalar.activation(
-                out=numer[:], in_=scores[t][:], func=ACT.Exp, bias=neg_max[:], scale=1.0, accum_out=totals[:, t : t + 1]
+                out=expd[t][:], in_=scores[t][:], func=ACT.Exp, bias=neg_max[:], accum_out=totals[:, t : t + 1]
             )
-            expd.append(numer)
-        for pair in range(TILES // 2):
-            inv = sb.tile([P, 2], F32, name=f"inv{pair}", tag="inv0" if pair == 0 else "expd0")
-            nc.vector.reciprocal(out=inv[:], in_=totals[:, 2 * pair : 2 * pair + 2])
-            for i in range(2):
-                t = 2 * pair + i
-                result = sb.tile([P, S], F32, name=f"result{t}")
-                nc.vector.scalar_tensor_tensor(
-                    out=result[:], in0=expd[t][:], scalar=inv[:, i : i + 1], in1=cs_picked[:], op0=ALU.mult, op1=ALU.mult
-                )
-                nc.sync.dma_start(out=out_rows[:, t, :], in_=result[:])
+
+        out_rows = out.rearrange("(p t) s -> p t s", t=TILES)
+
+        def finish(t, inv, first, last, queue):
+            result = tile([P, last - first], F32, f"result{t}_{first}")
+            nc.vector.scalar_tensor_tensor(
+                out=result[:],
+                in0=expd[t][:, first:last],
+                scalar=inv,
+                in1=cs_picked[:, first:last],
+                op0=ALU.mult,
+                op1=ALU.mult,
+            )
+            queue.dma_start(out=out_rows[:, t, first:last], in_=result[:])
+
+        inv01 = tile([P, 2], F32, "inv01")
+        nc.vector.reciprocal(out=inv01[:], in_=totals[:, 0:2])
+        finish(0, inv01[:, 0:1], 0, S, nc.sync)
+        inv23 = tile([P, 2], F32, "inv23", "expd0")
+        nc.vector.reciprocal(out=inv23[:], in_=totals[:, 2:4])
+        finish(1, inv01[:, 1:2], 0, S, nc.sync)
+        finish(2, inv23[:, 0:1], 0, S, nc.sync)
+        finish(3, inv23[:, 1:2], 0, HALF, nc.scalar)
+        finish(3, inv23[:, 1:2], HALF, S, nc.sync)

@@ -1,6 +1,7 @@
 from contextlib import ExitStack
 
 import concourse.mybir as mybir
+from concourse.masks import make_identity
 
 K, T, S, N, U = 1024, 2048, 512, 512, 512
 FLOPS = 2 * K * N * S
@@ -22,6 +23,11 @@ K_PASS = P * PACK
 TILES = N // P
 STRIPE = 16
 HALF = S // 2
+GROUP = 64
+GROUPS = N // GROUP
+SIDE = N // 2
+RUN = 8
+LINE = 4
 
 
 def tile_picked_sinkcol_none_p_kernel(tc, x_words, x_scales, w1, cs, offs, col, out):
@@ -41,44 +47,49 @@ def tile_picked_sinkcol_none_p_kernel(tc, x_words, x_scales, w1, cs, offs, col, 
         col_sb = lists.tile([P, S // STRIPE], U16, name="col_sb")
         scale_table = tile([P, T], U8, "scale_table")
         word_table = [tile([P, T], I32, f"word_table{z}") for z in range(2)]
-        w_raw = [tile([P, PACK, N], F32, f"w_raw{z}") for z in range(2)]
+        w_first = tile([P, PACK, N], F32, "w_first")
+        w_second = [tile([P, PACK, SIDE], F32, f"w_second{h}") for h in range(2)]
         cs_table = tile([P, U], F32, "cs_table")
+        identity = tile([P, P], F32, "identity")
 
-        nc.gpsimd.memset(scale_table[:, 0 : T // 2].bitcast(I32), 0)
-        nc.vector.memset(scale_table[:, T // 2 : T].bitcast(I32), 0)
+        nc.gpsimd.memset(cs_table[:, 0 : U // 2], 0.0)
+        nc.vector.memset(cs_table[:, U // 2 : U], 0.0)
+        nc.vector.memset(scale_table[:].bitcast(I32), 0)
+        make_identity(nc, identity[:])
 
-        def load_w(z):
-            rows = w1[z * K_PASS : (z + 1) * K_PASS, :]
-            nc.sync.dma_start(out=w_raw[z][:], in_=rows.rearrange("(p j) n -> p j n", j=PACK))
+        def load_w(raw, z, first, last):
+            rows = w1[z * K_PASS : (z + 1) * K_PASS, first:last]
+            nc.sync.dma_start(out=raw[:], in_=rows.rearrange("(p j) n -> p j n", j=PACK))
 
-        def load_scales(z):
-            for a in range(4):
-                nc.sync.dma_start(
-                    out=scale_table[4 * z + a : P : 32, :].bitcast(I32),
-                    in_=x_scales[z, a:16:4, :].bitcast(I32),
-                )
+        def load_scales(q):
+            nc.sync.dma_start(
+                out=scale_table[32 * q : 32 * q + 8, :].bitcast(I32),
+                in_=x_scales[:, 4 * q : 4 * q + 4, :].bitcast(I32),
+            )
 
         def load_words(z):
             nc.sync.dma_start(out=word_table[z][:], in_=x_words[z].rearrange("p c r -> p (c r)").bitcast(I32))
 
         nc.sync.dma_start(col_sb[:], col)
-        load_w(0)
         nc.sync.dma_start(offs_sb[:], offs)
-        nc.sync.dma_start(out=cs_table[:], in_=cs.rearrange("(p t) u -> p t u", t=TILES)[:, 0, :])
-        load_scales(0)
+        load_w(w_first, 0, 0, N)
+        nc.sync.dma_start(out=cs_table[0:P:STRIPE, :], in_=cs[0:N:GROUP, :])
+        for q in range(4):
+            load_scales(q)
         load_words(0)
-        load_scales(1)
-        load_w(1)
+        load_w(w_second[0], 1, 0, SIDE)
         load_words(1)
+        load_w(w_second[1], 1, SIDE, N)
 
-        def interleave(copy, grouped, raw, first, last):
-            dst = grouped[:].rearrange("p (t c j) -> p c j t", t=TILES, j=PACK)
-            src = raw[:].rearrange("p j (c t) -> p c j t", t=TILES)
-            copy(out=dst[:, first:last], in_=src[:, first:last])
+        def interleave(copy, grouped, place, raw, first, u):
+            dst = grouped[:, place * K_PASS : (place + 1) * K_PASS]
+            dst = dst.rearrange("p (a b i j) -> p a b j i", b=RUN // LINE, i=LINE, j=PACK)
+            src = raw[:, :, first : first + SIDE].rearrange("p j (a u b i) -> p u a b j i", u=2, b=RUN // LINE, i=LINE)
+            copy(out=dst, in_=src[:, u])
 
-        def quantize(grouped, name):
-            codes = tile([P, N], U32, f"{name}_codes")
-            plane = tile([P, N], U8, f"{name}_plane")
+        def quantize(grouped, width, name):
+            codes = tile([P, width], U32, f"{name}_codes")
+            plane = tile([P, width], U8, f"{name}_plane")
             nc.vector.quantize_mx(out=codes[:].bitcast(FP8X4), scales=plane[:], in_=grouped[:])
             return codes, plane
 
@@ -92,28 +103,51 @@ def tile_picked_sinkcol_none_p_kernel(tc, x_words, x_scales, w1, cs, offs, col, 
                 cs_picked[:, first : first + HALF], cs_table[:].indirect(entries(col_sb, first, first + HALF))
             )
 
-        grouped0 = tile([P, N * PACK], BF16, "grouped0")
-        interleave(nc.scalar.copy, grouped0, w_raw[0], 0, P)
-        w_quant0 = quantize(grouped0, "w0")
-
-        x_planes = tile([P, S], U8, "x_planes", "cs_table")
+        x_planes = tile([P, S], U8, "x_planes")
         nc.vector.tensor_copy(x_planes[:], scale_table[:].indirect(offs_sb[:]))
+
+        turned = psum.tile([P, S], F32, name="turned")
+        for c in range(S // P):
+            keys = slice(c * P, (c + 1) * P)
+            nc.tensor.transpose(turned[:, keys], cs_picked[:, keys], identity[:])
+
+        def regroup(raw, first, name):
+            grouped = tile([P, SIDE * PACK], BF16, name)
+            for u in range(2):
+                interleave(nc.scalar.copy, grouped, u, raw, first, u)
+            return grouped
+
+        def spread_factors(h):
+            spread = tile([P, S], F32, f"spread{h}")
+            one_each = turned[:].rearrange("p (c h g r) -> p h c g r", h=2, g=GROUPS // 2, r=STRIPE)[:, h, :, :, 0:1]
+            copies = P // (GROUPS // 2)
+            nc.scalar.copy(
+                out=spread[:].rearrange("p (c g r) -> p c g r", g=GROUPS // 2, r=copies),
+                in_=one_each.to_broadcast([P, S // P, GROUPS // 2, copies]),
+            )
+            bank = psum.tile([P, S], F32, name=f"factors{h}")
+            for c in range(S // P):
+                keys = slice(c * P, (c + 1) * P)
+                nc.tensor.transpose(bank[:, keys], spread[:, keys], identity[:])
+            return bank
+
+        grouped0 = [regroup(w_first, h * SIDE, f"grouped0{h}") for h in range(2)]
+        w_quant0 = [quantize(grouped0[0], SIDE, "w00")]
 
         x_codes = [tile([P, S], U32, f"x_codes{z}") for z in range(2)]
         pick_words(0, x_codes[0], 0, S)
+        w_quant0.append(quantize(grouped0[1], SIDE, "w01"))
+        factors = [spread_factors(0)]
 
-        grouped1 = tile([P, N * PACK], BF16, "grouped1", "scale_table")
-        interleave(nc.scalar.copy, grouped1, w_raw[1], 0, P // 2)
-        interleave(nc.vector.tensor_copy, grouped1, w_raw[1], P // 2, P)
-        w_quant1 = quantize(grouped1, "w1")
+        w_quant1 = quantize(regroup(w_second[0], 0, "grouped1"), SIDE, "w1")
         pick_words(1, x_codes[1], 0, HALF)
         pick_words(1, x_codes[1], HALF, S)
 
         scores = [psum.tile([P, S], F32, name=f"scores{t}") for t in range(TILES)]
 
-        def multiply(t, z, w_quant, first, last):
+        def multiply(t, z, w_quant, place, first, last):
             codes, plane = w_quant
-            queries = slice(t * P, (t + 1) * P)
+            queries = slice(place * P, (place + 1) * P)
             nc.tensor.matmul_mx(
                 out=scores[t][:, first:last],
                 lhsT=codes[:, queries].bitcast(FP8X4),
@@ -125,16 +159,17 @@ def tile_picked_sinkcol_none_p_kernel(tc, x_words, x_scales, w1, cs, offs, col, 
             )
 
         for t in range(TILES):
-            multiply(t, 0, w_quant0, 0, S)
+            multiply(t, 0, w_quant0[t // 2], t % 2, 0, S)
         for first in (0, HALF):
-            for t in range(TILES // 2):
-                multiply(t, 1, w_quant1, first, first + HALF)
-        for t in range(TILES // 2, TILES):
-            multiply(t, 1, w_quant1, 0, S)
+            for t in range(2):
+                multiply(t, 1, w_quant1, t, first, first + HALF)
+
+        factors.append(spread_factors(1))
 
         totals = tile([P, TILES], F32, "totals")
         expd = []
-        for t in range(TILES):
+
+        def exponentiate(t):
             neg_max = tile([P, 1], F32, f"neg_max{t}")
             nc.vector.tensor_reduce(out=neg_max[:], in_=scores[t][:], axis=AX.X, op=ALU.max, negate=True)
             expd.append(tile([P, S], F32, f"expd{t}"))
@@ -142,26 +177,36 @@ def tile_picked_sinkcol_none_p_kernel(tc, x_words, x_scales, w1, cs, offs, col, 
                 out=expd[t][:], in_=scores[t][:], func=ACT.Exp, bias=neg_max[:], accum_out=totals[:, t : t + 1]
             )
 
-        out_rows = out.rearrange("(p t) s -> p t s", t=TILES)
+        def invert(t):
+            inv = tile([P, 1], F32, f"inv{t}")
+            nc.vector.reciprocal(out=inv[:], in_=totals[:, t : t + 1])
+            return inv
 
-        def finish(t, inv, first, last, queue):
-            result = tile([P, last - first], F32, f"result{t}_{first}")
+        out_rows = out.rearrange("(h a u i) s -> h u a i s", h=2, u=2, i=RUN)
+
+        def finish(t, inv):
+            result = tile([P, S], F32, f"result{t}")
             nc.vector.scalar_tensor_tensor(
-                out=result[:],
-                in0=expd[t][:, first:last],
-                scalar=inv,
-                in1=cs_picked[:, first:last],
-                op0=ALU.mult,
-                op1=ALU.mult,
+                out=result[:], in0=expd[t][:], scalar=inv[:], in1=factors[t // 2][:], op0=ALU.mult, op1=ALU.mult
             )
-            queue.dma_start(out=out_rows[:, t, first:last], in_=result[:])
+            nc.sync.dma_start(out=out_rows[t // 2, t % 2], in_=result[:])
 
-        inv01 = tile([P, 2], F32, "inv01")
-        nc.vector.reciprocal(out=inv01[:], in_=totals[:, 0:2])
-        finish(0, inv01[:, 0:1], 0, S, nc.sync)
-        inv23 = tile([P, 2], F32, "inv23", "expd0")
-        nc.vector.reciprocal(out=inv23[:], in_=totals[:, 2:4])
-        finish(1, inv01[:, 1:2], 0, S, nc.sync)
-        finish(2, inv23[:, 0:1], 0, S, nc.sync)
-        finish(3, inv23[:, 1:2], 0, HALF, nc.scalar)
-        finish(3, inv23[:, 1:2], HALF, S, nc.sync)
+        late = []
+        for u in range(2):
+            late.append(tile([P, K_PASS], BF16, f"late{u}"))
+            interleave(nc.scalar.copy, late[u], 0, w_second[1], 0, u)
+
+        exponentiate(0)
+        exponentiate(1)
+        multiply(2, 1, quantize(late[0], P, "w2"), 0, 0, S)
+        inv0 = invert(0)
+        multiply(3, 1, quantize(late[1], P, "w3"), 0, 0, S)
+        finish(0, inv0)
+        inv1 = invert(1)
+        exponentiate(2)
+        exponentiate(3)
+        inv2 = invert(2)
+        finish(1, inv1)
+        inv3 = invert(3)
+        finish(2, inv2)
+        finish(3, inv3)

@@ -25,9 +25,7 @@ STRIPE = 16
 HALF = S // 2
 GROUP = 64
 GROUPS = N // GROUP
-SIDE = N // 2
 RUN = 8
-LINE = 4
 
 
 def tile_picked_sinkcol_none_p_kernel(tc, x_words, x_scales, w1, cs, offs, col, out):
@@ -47,8 +45,7 @@ def tile_picked_sinkcol_none_p_kernel(tc, x_words, x_scales, w1, cs, offs, col, 
         col_sb = lists.tile([P, S // STRIPE], U16, name="col_sb")
         scale_table = tile([P, T], U8, "scale_table")
         word_table = [tile([P, T], I32, f"word_table{z}") for z in range(2)]
-        w_first = tile([P, PACK, N], F32, "w_first")
-        w_second = [tile([P, PACK, SIDE], F32, f"w_second{h}") for h in range(2)]
+        w_raw = [tile([P, PACK, N], F32, f"w_raw{z}") for z in range(2)]
         cs_table = tile([P, U], F32, "cs_table")
         identity = tile([P, P], F32, "identity")
 
@@ -56,42 +53,50 @@ def tile_picked_sinkcol_none_p_kernel(tc, x_words, x_scales, w1, cs, offs, col, 
         nc.vector.memset(cs_table[:, U // 2 : U], 0.0)
         nc.vector.memset(scale_table[:].bitcast(I32), 0)
         make_identity(nc, identity[:])
+        minus_one = tile([P, 1], F32, "minus_one")
+        nc.gpsimd.memset(minus_one[:], -1.0)
 
-        def load_w(raw, z, first, last):
-            rows = w1[z * K_PASS : (z + 1) * K_PASS, first:last]
-            nc.sync.dma_start(out=raw[:], in_=rows.rearrange("(p j) n -> p j n", j=PACK))
+        def load_w(z):
+            rows = w1[z * K_PASS : (z + 1) * K_PASS, :]
+            nc.sync.dma_start(out=w_raw[z][:], in_=rows.rearrange("(p j) n -> p j n", j=PACK))
 
-        def load_scales(q):
-            nc.sync.dma_start(
-                out=scale_table[32 * q : 32 * q + 8, :].bitcast(I32),
-                in_=x_scales[:, 4 * q : 4 * q + 4, :].bitcast(I32),
-            )
+        def load_scales(z):
+            for a in range(4):
+                nc.sync.dma_start(
+                    out=scale_table[4 * z + a : P : 32, :].bitcast(I32),
+                    in_=x_scales[z, a:16:4, :].bitcast(I32),
+                )
 
         def load_words(z):
             nc.sync.dma_start(out=word_table[z][:], in_=x_words[z].rearrange("p c r -> p (c r)").bitcast(I32))
 
         nc.sync.dma_start(col_sb[:], col)
+        load_w(0)
         nc.sync.dma_start(offs_sb[:], offs)
-        load_w(w_first, 0, 0, N)
         nc.sync.dma_start(out=cs_table[0:P:STRIPE, :], in_=cs[0:N:GROUP, :])
-        for q in range(4):
-            load_scales(q)
+        load_scales(0)
         load_words(0)
-        load_w(w_second[0], 1, 0, SIDE)
+        load_scales(1)
+        load_w(1)
         load_words(1)
-        load_w(w_second[1], 1, SIDE, N)
 
-        def interleave(copy, grouped, place, raw, first, u):
-            dst = grouped[:, place * K_PASS : (place + 1) * K_PASS]
-            dst = dst.rearrange("p (a b i j) -> p a b j i", b=RUN // LINE, i=LINE, j=PACK)
-            src = raw[:, :, first : first + SIDE].rearrange("p j (a u b i) -> p u a b j i", u=2, b=RUN // LINE, i=LINE)
-            copy(out=dst, in_=src[:, u])
+        def regroup(copy, z, pair):
+            grouped = tile([P, 2 * K_PASS], BF16, f"grouped{z}{pair}")
+            dst = grouped[:].rearrange("p (u a i j) -> p u a i j", u=2, i=RUN, j=PACK)
+            src = w_raw[z][:].rearrange("p j (a t i) -> p t a i j", t=TILES, i=RUN)
+            copy(out=dst, in_=src[:, 2 * pair : 2 * pair + 2])
+            return grouped
 
-        def quantize(grouped, width, name):
-            codes = tile([P, width], U32, f"{name}_codes")
-            plane = tile([P, width], U8, f"{name}_plane")
+        def quantize(grouped, name):
+            codes = tile([P, 2 * P], U32, f"{name}_codes")
+            plane = tile([P, 2 * P], U8, f"{name}_plane")
             nc.vector.quantize_mx(out=codes[:].bitcast(FP8X4), scales=plane[:], in_=grouped[:])
             return codes, plane
+
+        def quantize_pass(z):
+            by_scalar = regroup(nc.scalar.copy, z, 0)
+            second = quantize(regroup(nc.vector.tensor_copy, z, 1), f"w{z}1")
+            return [quantize(by_scalar, f"w{z}0"), second]
 
         def pick_words(z, picked, first, last):
             window = word_table[z][:].bitcast(U32)
@@ -103,110 +108,110 @@ def tile_picked_sinkcol_none_p_kernel(tc, x_words, x_scales, w1, cs, offs, col, 
                 cs_picked[:, first : first + HALF], cs_table[:].indirect(entries(col_sb, first, first + HALF))
             )
 
-        x_planes = tile([P, S], U8, "x_planes")
-        nc.vector.tensor_copy(x_planes[:], scale_table[:].indirect(offs_sb[:]))
-
-        turned = psum.tile([P, S], F32, name="turned")
-        for c in range(S // P):
-            keys = slice(c * P, (c + 1) * P)
-            nc.tensor.transpose(turned[:, keys], cs_picked[:, keys], identity[:])
-
-        def regroup(raw, first, name):
-            grouped = tile([P, SIDE * PACK], BF16, name)
-            for u in range(2):
-                interleave(nc.scalar.copy, grouped, u, raw, first, u)
-            return grouped
-
-        def spread_factors(h):
-            spread = tile([P, S], F32, f"spread{h}")
-            one_each = turned[:].rearrange("p (c h g r) -> p h c g r", h=2, g=GROUPS // 2, r=STRIPE)[:, h, :, :, 0:1]
-            copies = P // (GROUPS // 2)
-            nc.scalar.copy(
-                out=spread[:].rearrange("p (c g r) -> p c g r", g=GROUPS // 2, r=copies),
-                in_=one_each.to_broadcast([P, S // P, GROUPS // 2, copies]),
-            )
-            bank = psum.tile([P, S], F32, name=f"factors{h}")
+        def turn(source, name):
+            bank = psum.tile([P, S], F32, name=name)
             for c in range(S // P):
                 keys = slice(c * P, (c + 1) * P)
-                nc.tensor.transpose(bank[:, keys], spread[:, keys], identity[:])
+                nc.tensor.transpose(bank[:, keys], source[:, keys], identity[:])
             return bank
 
-        grouped0 = [regroup(w_first, h * SIDE, f"grouped0{h}") for h in range(2)]
-        w_quant0 = [quantize(grouped0[0], SIDE, "w00")]
+        turned = turn(cs_picked, "turned")
+        w_quant = [quantize_pass(0)]
+
+        spread = tile([P, S], F32, "spread")
+        one_each = turned[:].rearrange("p (c r) -> p c r", r=STRIPE)[:, :, 0:1]
+        nc.scalar.copy(
+            out=spread[:].rearrange("p (c r) -> p c r", r=STRIPE), in_=one_each.to_broadcast([P, S // STRIPE, STRIPE])
+        )
+        factors = turn(spread, "factors")
 
         x_codes = [tile([P, S], U32, f"x_codes{z}") for z in range(2)]
         pick_words(0, x_codes[0], 0, S)
-        w_quant0.append(quantize(grouped0[1], SIDE, "w01"))
-        factors = [spread_factors(0)]
-
-        w_quant1 = quantize(regroup(w_second[0], 0, "grouped1"), SIDE, "w1")
+        x_planes = tile([P, S], U8, "x_planes")
+        nc.vector.tensor_copy(x_planes[:], scale_table[:].indirect(offs_sb[:]))
+        w_quant.append(quantize_pass(1))
         pick_words(1, x_codes[1], 0, HALF)
         pick_words(1, x_codes[1], HALF, S)
 
-        scores = [psum.tile([P, S], F32, name=f"scores{t}") for t in range(TILES)]
-
-        def multiply(t, z, w_quant, place, first, last):
-            codes, plane = w_quant
-            queries = slice(place * P, (place + 1) * P)
+        def multiply(bank, t, z, first, last):
+            codes, plane = w_quant[z][t // 2]
+            queries = slice(t % 2 * P, (t % 2 + 1) * P)
             nc.tensor.matmul_mx(
-                out=scores[t][:, first:last],
+                out=bank[:],
                 lhsT=codes[:, queries].bitcast(FP8X4),
                 lhsT_scale=plane[:, queries],
                 rhs=x_codes[z][:, first:last].bitcast(FP8X4),
                 rhs_scale=x_planes[4 * z : P, first:last],
                 start=(z == 0),
-                stop=(z == 1 and last == S),
+                stop=(z == 1),
             )
 
-        for t in range(TILES):
-            multiply(t, 0, w_quant0[t // 2], t % 2, 0, S)
-        for first in (0, HALF):
-            for t in range(2):
-                multiply(t, 1, w_quant1, t, first, first + HALF)
-
-        factors.append(spread_factors(1))
+        pieces = [(t, first, first + HALF) for first in (0, HALF) for t in range(2)]
+        pieces = pieces + [(t, 0, S) for t in range(2, TILES)]
+        scores = {(t, a): psum.tile([P, b - a], F32, name=f"scores{t}_{a}") for t, a, b in pieces}
+        for z in range(2):
+            for t, a, b in pieces:
+                multiply(scores[t, a], t, z, a, b)
 
         totals = tile([P, TILES], F32, "totals")
-        expd = []
+        expd = [tile([P, S], F32, f"expd{t}") for t in range(TILES)]
+        negated = [tile([P, S], F32, f"negated{t}") for t in range(2)]
+        least = {}
+        for t, a, b in pieces[:4]:
+            least[t, a] = tile([P, 1], F32, f"least{t}_{a}")
+            nc.vector.tensor_scalar(
+                out=negated[t][:, a:b],
+                in0=scores[t, a][:],
+                scalar1=-1.0,
+                scalar2=None if a == 0 else least[t, 0][:],
+                op0=ALU.mult,
+                op1=ALU.min,
+                accum_out=least[t, a][:],
+            )
+        for t in range(2):
+            nc.scalar.activation(
+                out=expd[t][:],
+                in_=negated[t][:],
+                func=ACT.Exp,
+                scale=-1.0,
+                bias=least[t, HALF][:],
+                accum_out=totals[:, t : t + 1],
+            )
 
         def exponentiate(t):
             neg_max = tile([P, 1], F32, f"neg_max{t}")
-            nc.vector.tensor_reduce(out=neg_max[:], in_=scores[t][:], axis=AX.X, op=ALU.max, negate=True)
-            expd.append(tile([P, S], F32, f"expd{t}"))
+            nc.vector.tensor_reduce(out=neg_max[:], in_=scores[t, 0][:], axis=AX.X, op=ALU.max, negate=True)
             nc.scalar.activation(
-                out=expd[t][:], in_=scores[t][:], func=ACT.Exp, bias=neg_max[:], accum_out=totals[:, t : t + 1]
+                out=expd[t][:], in_=scores[t, 0][:], func=ACT.Exp, bias=neg_max[:], accum_out=totals[:, t : t + 1]
             )
 
         def invert(t):
             inv = tile([P, 1], F32, f"inv{t}")
-            nc.vector.reciprocal(out=inv[:], in_=totals[:, t : t + 1])
+            nc.gpsimd.tensor_tensor(out=inv[:], in0=totals[:, t : t + 1], in1=minus_one[:], op=ALU.pow)
             return inv
 
-        out_rows = out.rearrange("(h a u i) s -> h u a i s", h=2, u=2, i=RUN)
+        out_rows = out.rearrange("(a t i) s -> t a i s", t=TILES, i=RUN)
 
-        def finish(t, inv):
-            result = tile([P, S], F32, f"result{t}")
+        def finish(t, inv, first, last, queue):
+            result = tile([P, last - first], F32, f"result{t}_{first}")
             nc.vector.scalar_tensor_tensor(
-                out=result[:], in0=expd[t][:], scalar=inv[:], in1=factors[t // 2][:], op0=ALU.mult, op1=ALU.mult
+                out=result[:],
+                in0=expd[t][:, first:last],
+                scalar=inv[:],
+                in1=factors[:, first:last],
+                op0=ALU.mult,
+                op1=ALU.mult,
             )
-            nc.sync.dma_start(out=out_rows[t // 2, t % 2], in_=result[:])
+            queue.dma_start(out=out_rows[t, :, :, first:last], in_=result[:])
 
-        late = []
-        for u in range(2):
-            late.append(tile([P, K_PASS], BF16, f"late{u}"))
-            interleave(nc.scalar.copy, late[u], 0, w_second[1], 0, u)
-
-        exponentiate(0)
-        exponentiate(1)
-        multiply(2, 1, quantize(late[0], P, "w2"), 0, 0, S)
-        inv0 = invert(0)
-        multiply(3, 1, quantize(late[1], P, "w3"), 0, 0, S)
-        finish(0, inv0)
-        inv1 = invert(1)
         exponentiate(2)
+        inv0 = invert(0)
         exponentiate(3)
+        inv1 = invert(1)
+        finish(0, inv0, 0, S, nc.sync)
         inv2 = invert(2)
-        finish(1, inv1)
+        finish(1, inv1, 0, S, nc.sync)
         inv3 = invert(3)
-        finish(2, inv2)
-        finish(3, inv3)
+        finish(2, inv2, 0, S, nc.sync)
+        finish(3, inv3, 0, HALF, nc.scalar)
+        finish(3, inv3, HALF, S, nc.sync)

@@ -26,6 +26,7 @@ HALF = S // 2
 GROUP = 64
 GROUPS = N // GROUP
 RUN = 8
+CS_ROW = 8
 
 
 def tile_picked_sinkcol_none_p_kernel(tc, x_words, x_scales, w1, cs, offs, col, out):
@@ -60,12 +61,13 @@ def tile_picked_sinkcol_none_p_kernel(tc, x_words, x_scales, w1, cs, offs, col, 
             rows = w1[z * K_PASS : (z + 1) * K_PASS, :]
             nc.sync.dma_start(out=w_raw[z][:], in_=rows.rearrange("(p j) n -> p j n", j=PACK))
 
-        def load_scales(z):
-            for a in range(4):
-                nc.sync.dma_start(
-                    out=scale_table[4 * z + a : P : 32, :].bitcast(I32),
-                    in_=x_scales[z, a:16:4, :].bitcast(I32),
-                )
+        def load_scales(pair):
+            for a in (2 * pair, 2 * pair + 1):
+                for z in range(2):
+                    nc.sync.dma_start(
+                        out=scale_table[4 * z + a : P : 32, :].bitcast(I32),
+                        in_=x_scales[z, a:16:4, :].bitcast(I32),
+                    )
 
         def load_words(z):
             nc.sync.dma_start(out=word_table[z][:], in_=x_words[z].rearrange("p c r -> p (c r)").bitcast(I32))
@@ -73,7 +75,7 @@ def tile_picked_sinkcol_none_p_kernel(tc, x_words, x_scales, w1, cs, offs, col, 
         nc.sync.dma_start(col_sb[:], col)
         load_w(0)
         nc.sync.dma_start(offs_sb[:], offs)
-        nc.sync.dma_start(out=cs_table[0:P:STRIPE, :], in_=cs[0:N:GROUP, :])
+        nc.sync.dma_start(out=cs_table[CS_ROW:P:STRIPE, :], in_=cs[0:N:GROUP, :])
         load_scales(0)
         load_words(0)
         load_scales(1)
@@ -119,7 +121,7 @@ def tile_picked_sinkcol_none_p_kernel(tc, x_words, x_scales, w1, cs, offs, col, 
         w_quant = [quantize_pass(0)]
 
         spread = tile([P, S], F32, "spread")
-        one_each = turned[:].rearrange("p (c r) -> p c r", r=STRIPE)[:, :, 0:1]
+        one_each = turned[:].rearrange("p (c r) -> p c r", r=STRIPE)[:, :, CS_ROW : CS_ROW + 1]
         nc.scalar.copy(
             out=spread[:].rearrange("p (c r) -> p c r", r=STRIPE), in_=one_each.to_broadcast([P, S // STRIPE, STRIPE])
         )

@@ -215,5 +215,4 @@ def tile_picked_sinkcol_none_p_kernel(tc, x_words, x_scales, w1, cs, offs, col, 
         finish(1, inv1, 0, S, nc.sync)
         inv3 = invert(3)
         finish(2, inv2, 0, S, nc.sync)
-        finish(3, inv3, 0, HALF, nc.scalar)
-        finish(3, inv3, HALF, S, nc.sync)
+        finish(3, inv3, 0, S, nc.sync)

@@ -20,13 +20,17 @@ AX = mybir.AxisListType
 P = 128
 PACK = 4
 K_PASS = P * PACK
+PASSES = K // K_PASS
 TILES = N // P
+SPLIT_TILES = 2
 STRIPE = 16
 HALF = S // 2
 GROUP = 64
-GROUPS = N // GROUP
 RUN = 8
+QUADRANT = 32
+SCALE_ROWS = 4
 CS_ROW = 8
+SCALES_AHEAD = 3
 
 
 def tile_picked_sinkcol_none_p_kernel(tc, x_words, x_scales, w1, cs, offs, col, out):
@@ -36,8 +40,8 @@ def tile_picked_sinkcol_none_p_kernel(tc, x_words, x_scales, w1, cs, offs, col, 
         sb = ctx.enter_context(tc.tile_pool(name="sb", bufs=1))
         psum = ctx.enter_context(tc.psum_pool(name="psum", bufs=1))
 
-        def tile(shape, dtype, name, slot=None):
-            return sb.tile(shape, dtype, name=name, tag=slot or name, align_bytes=64)
+        def tile(shape, dtype, name):
+            return sb.tile(shape, dtype, name=name, tag=name, align_bytes=64)
 
         def entries(list_tile, first, last):
             return list_tile[:, first // STRIPE : last // STRIPE]
@@ -45,8 +49,8 @@ def tile_picked_sinkcol_none_p_kernel(tc, x_words, x_scales, w1, cs, offs, col, 
         offs_sb = lists.tile([P, S // STRIPE], U16, name="offs_sb")
         col_sb = lists.tile([P, S // STRIPE], U16, name="col_sb")
         scale_table = tile([P, T], U8, "scale_table")
-        word_table = [tile([P, T], I32, f"word_table{z}") for z in range(2)]
-        w_raw = [tile([P, PACK, N], F32, f"w_raw{z}") for z in range(2)]
+        word_table = [tile([P, T], I32, f"word_table{z}") for z in range(PASSES)]
+        w_raw = [tile([P, PACK, N], F32, f"w_raw{z}") for z in range(PASSES)]
         cs_table = tile([P, U], F32, "cs_table")
         identity = tile([P, P], F32, "identity")
 
@@ -61,24 +65,24 @@ def tile_picked_sinkcol_none_p_kernel(tc, x_words, x_scales, w1, cs, offs, col, 
             rows = w1[z * K_PASS : (z + 1) * K_PASS, :]
             nc.sync.dma_start(out=w_raw[z][:], in_=rows.rearrange("(p j) n -> p j n", j=PACK))
 
-        def load_scales(pair):
-            for a in (2 * pair, 2 * pair + 1):
-                for z in range(2):
-                    nc.sync.dma_start(
-                        out=scale_table[4 * z + a : P : 32, :].bitcast(I32),
-                        in_=x_scales[z, a:16:4, :].bitcast(I32),
-                    )
+        def load_scales(rows):
+            for a, z in rows:
+                nc.sync.dma_start(
+                    out=scale_table[SCALE_ROWS * z + a : P : QUADRANT, :].bitcast(I32),
+                    in_=x_scales[z, a :: SCALE_ROWS, :].bitcast(I32),
+                )
 
         def load_words(z):
             nc.sync.dma_start(out=word_table[z][:], in_=x_words[z].rearrange("p c r -> p (c r)").bitcast(I32))
 
-        nc.sync.dma_start(col_sb[:], col)
+        scale_rows = [(a, z) for a in range(SCALE_ROWS) for z in range(PASSES)]
         load_w(0)
+        nc.sync.dma_start(col_sb[:], col)
         nc.sync.dma_start(offs_sb[:], offs)
         nc.sync.dma_start(out=cs_table[CS_ROW:P:STRIPE, :], in_=cs[0:N:GROUP, :])
-        load_scales(0)
+        load_scales(scale_rows[:SCALES_AHEAD])
         load_words(0)
-        load_scales(1)
+        load_scales(scale_rows[SCALES_AHEAD:])
         load_w(1)
         load_words(1)
 
@@ -100,23 +104,22 @@ def tile_picked_sinkcol_none_p_kernel(tc, x_words, x_scales, w1, cs, offs, col, 
             second = quantize(regroup(nc.vector.tensor_copy, z, 1), f"w{z}1")
             return [quantize(by_scalar, f"w{z}0"), second]
 
-        def pick_words(z, picked, first, last):
+        def pick_words(z, first, last):
             window = word_table[z][:].bitcast(U32)
-            nc.vector.tensor_copy(picked[:, first:last], window.indirect(entries(offs_sb, first, last)))
+            nc.vector.tensor_copy(x_codes[z][:, first:last], window.indirect(entries(offs_sb, first, last)))
+
+        def turn(source, name):
+            bank = psum.tile([P, S], F32, name=name)
+            for c in range(S // P):
+                block = slice(c * P, (c + 1) * P)
+                nc.tensor.transpose(bank[:, block], source[:, block], identity[:])
+            return bank
 
         cs_picked = tile([P, S], F32, "cs_picked")
         for first in (0, HALF):
             nc.vector.tensor_copy(
                 cs_picked[:, first : first + HALF], cs_table[:].indirect(entries(col_sb, first, first + HALF))
             )
-
-        def turn(source, name):
-            bank = psum.tile([P, S], F32, name=name)
-            for c in range(S // P):
-                keys = slice(c * P, (c + 1) * P)
-                nc.tensor.transpose(bank[:, keys], source[:, keys], identity[:])
-            return bank
-
         turned = turn(cs_picked, "turned")
         w_quant = [quantize_pass(0)]
 
@@ -127,13 +130,13 @@ def tile_picked_sinkcol_none_p_kernel(tc, x_words, x_scales, w1, cs, offs, col, 
         )
         factors = turn(spread, "factors")
 
-        x_codes = [tile([P, S], U32, f"x_codes{z}") for z in range(2)]
-        pick_words(0, x_codes[0], 0, S)
+        x_codes = [tile([P, S], U32, f"x_codes{z}") for z in range(PASSES)]
+        pick_words(0, 0, S)
         x_planes = tile([P, S], U8, "x_planes")
         nc.vector.tensor_copy(x_planes[:], scale_table[:].indirect(offs_sb[:]))
         w_quant.append(quantize_pass(1))
-        pick_words(1, x_codes[1], 0, HALF)
-        pick_words(1, x_codes[1], HALF, S)
+        pick_words(1, 0, HALF)
+        pick_words(1, HALF, S)
 
         def multiply(bank, t, z, first, last):
             codes, plane = w_quant[z][t // 2]
@@ -143,34 +146,34 @@ def tile_picked_sinkcol_none_p_kernel(tc, x_words, x_scales, w1, cs, offs, col, 
                 lhsT=codes[:, queries].bitcast(FP8X4),
                 lhsT_scale=plane[:, queries],
                 rhs=x_codes[z][:, first:last].bitcast(FP8X4),
-                rhs_scale=x_planes[4 * z : P, first:last],
+                rhs_scale=x_planes[SCALE_ROWS * z : P, first:last],
                 start=(z == 0),
-                stop=(z == 1),
+                stop=(z == PASSES - 1),
             )
 
-        pieces = [(t, first, first + HALF) for first in (0, HALF) for t in range(2)]
-        pieces = pieces + [(t, 0, S) for t in range(2, TILES)]
-        scores = {(t, a): psum.tile([P, b - a], F32, name=f"scores{t}_{a}") for t, a, b in pieces}
-        for z in range(2):
-            for t, a, b in pieces:
-                multiply(scores[t, a], t, z, a, b)
+        halves = [(t, first, first + HALF) for first in (0, HALF) for t in range(SPLIT_TILES)]
+        pieces = halves + [(t, 0, S) for t in range(SPLIT_TILES, TILES)]
+        scores = {(t, first): psum.tile([P, last - first], F32, name=f"scores{t}_{first}") for t, first, last in pieces}
+        for z in range(PASSES):
+            for t, first, last in pieces:
+                multiply(scores[t, first], t, z, first, last)
 
         totals = tile([P, TILES], F32, "totals")
         expd = [tile([P, S], F32, f"expd{t}") for t in range(TILES)]
-        negated = [tile([P, S], F32, f"negated{t}") for t in range(2)]
+        negated = [tile([P, S], F32, f"negated{t}") for t in range(SPLIT_TILES)]
         least = {}
-        for t, a, b in pieces[:4]:
-            least[t, a] = tile([P, 1], F32, f"least{t}_{a}")
+        for t, first, last in halves:
+            least[t, first] = tile([P, 1], F32, f"least{t}_{first}")
             nc.vector.tensor_scalar(
-                out=negated[t][:, a:b],
-                in0=scores[t, a][:],
+                out=negated[t][:, first:last],
+                in0=scores[t, first][:],
                 scalar1=-1.0,
-                scalar2=None if a == 0 else least[t, 0][:],
+                scalar2=None if first == 0 else least[t, 0][:],
                 op0=ALU.mult,
                 op1=ALU.min,
-                accum_out=least[t, a][:],
+                accum_out=least[t, first][:],
             )
-        for t in range(2):
+        for t in range(SPLIT_TILES):
             nc.scalar.activation(
                 out=expd[t][:],
                 in_=negated[t][:],
@@ -194,25 +197,14 @@ def tile_picked_sinkcol_none_p_kernel(tc, x_words, x_scales, w1, cs, offs, col, 
 
         out_rows = out.rearrange("(a t i) s -> t a i s", t=TILES, i=RUN)
 
-        def finish(t, inv, first, last, queue):
-            result = tile([P, last - first], F32, f"result{t}_{first}")
+        def finish(t, inv):
+            result = tile([P, S], F32, f"result{t}")
             nc.vector.scalar_tensor_tensor(
-                out=result[:],
-                in0=expd[t][:, first:last],
-                scalar=inv[:],
-                in1=factors[:, first:last],
-                op0=ALU.mult,
-                op1=ALU.mult,
+                out=result[:], in0=expd[t][:], scalar=inv[:], in1=factors[:], op0=ALU.mult, op1=ALU.mult
             )
-            queue.dma_start(out=out_rows[t, :, :, first:last], in_=result[:])
+            nc.sync.dma_start(out=out_rows[t], in_=result[:])
 
-        exponentiate(2)
-        inv0 = invert(0)
-        exponentiate(3)
-        inv1 = invert(1)
-        finish(0, inv0, 0, S, nc.sync)
-        inv2 = invert(2)
-        finish(1, inv1, 0, S, nc.sync)
-        inv3 = invert(3)
-        finish(2, inv2, 0, S, nc.sync)
-        finish(3, inv3, 0, S, nc.sync)
+        for t in range(SPLIT_TILES, TILES):
+            exponentiate(t)
+        for t in range(TILES):
+            finish(t, invert(t))

@@ -50,7 +50,8 @@ def tile_picked_sinkcol_none_p_kernel(tc, x_words, x_scales, w1, cs, offs, col, 
         col_sb = lists.tile([P, S // STRIPE], U16, name="col_sb")
         scale_table = tile([P, T], U8, "scale_table")
         word_table = [tile([P, T], I32, f"word_table{z}") for z in range(PASSES)]
-        w_raw = [tile([P, PACK, N], F32, f"w_raw{z}") for z in range(PASSES)]
+        w_first = tile([P, PACK, N], F32, "w_first")
+        w_second = [tile([P, PACK, N // 2], F32, f"w_second{h}") for h in range(2)]
         cs_table = tile([P, U], F32, "cs_table")
         identity = tile([P, P], F32, "identity")
 
@@ -61,9 +62,9 @@ def tile_picked_sinkcol_none_p_kernel(tc, x_words, x_scales, w1, cs, offs, col, 
         minus_one = tile([P, 1], F32, "minus_one")
         nc.gpsimd.memset(minus_one[:], -1.0)
 
-        def load_w(z):
-            rows = w1[z * K_PASS : (z + 1) * K_PASS, :]
-            nc.sync.dma_start(out=w_raw[z][:], in_=rows.rearrange("(p j) n -> p j n", j=PACK))
+        def load_w(raw, z, first, last):
+            rows = w1[z * K_PASS : (z + 1) * K_PASS, first:last]
+            nc.sync.dma_start(out=raw[:], in_=rows.rearrange("(p j) n -> p j n", j=PACK))
 
         def load_scales(rows):
             for a, z in rows:
@@ -76,40 +77,36 @@ def tile_picked_sinkcol_none_p_kernel(tc, x_words, x_scales, w1, cs, offs, col, 
             nc.sync.dma_start(out=word_table[z][:], in_=x_words[z].rearrange("p c r -> p (c r)").bitcast(I32))
 
         scale_rows = [(a, z) for a in range(SCALE_ROWS) for z in range(PASSES)]
-        load_w(0)
+        load_w(w_first, 0, 0, N)
         nc.sync.dma_start(col_sb[:], col)
         nc.sync.dma_start(offs_sb[:], offs)
         nc.sync.dma_start(out=cs_table[CS_ROW:P:STRIPE, :], in_=cs[0:N:GROUP, :])
         load_scales(scale_rows[:SCALES_AHEAD])
         load_words(0)
         load_scales(scale_rows[SCALES_AHEAD:])
-        load_w(1)
+        load_w(w_second[0], 1, 0, N // 2)
         load_words(1)
+        load_w(w_second[1], 1, N // 2, N)
 
-        def regroup(copy, z, pair):
-            grouped = tile([P, 2 * K_PASS], BF16, f"grouped{z}{pair}")
-            dst = grouped[:].rearrange("p (u a i j) -> p u a i j", u=2, i=RUN, j=PACK)
-            src = w_raw[z][:].rearrange("p j (a t i) -> p t a i j", t=TILES, i=RUN)
-            copy(out=dst, in_=src[:, 2 * pair : 2 * pair + 2])
+        def regroup(copy, raw, first, last, name):
+            grouped = tile([P, (last - first) * K_PASS], BF16, name)
+            dst = grouped[:].rearrange("p (u a i j) -> p u a i j", u=last - first, i=RUN, j=PACK)
+            src = raw.rearrange("p j (a u i) -> p u a i j", u=2, i=RUN)
+            copy(out=dst, in_=src[:, first:last])
             return grouped
 
-        def quantize(grouped, name):
-            codes = tile([P, 2 * P], U32, f"{name}_codes")
-            plane = tile([P, 2 * P], U8, f"{name}_plane")
+        def quantize(grouped, width, name):
+            codes = tile([P, width], U32, f"{name}_codes")
+            plane = tile([P, width], U8, f"{name}_plane")
             nc.vector.quantize_mx(out=codes[:].bitcast(FP8X4), scales=plane[:], in_=grouped[:])
-            return codes, plane
-
-        def quantize_pass(z):
-            by_scalar = regroup(nc.scalar.copy, z, 0)
-            second = quantize(regroup(nc.vector.tensor_copy, z, 1), f"w{z}1")
-            return [quantize(by_scalar, f"w{z}0"), second]
+            return [(codes[:, c : c + P], plane[:, c : c + P]) for c in range(0, width, P)]
 
         def pick_words(z, first, last):
             window = word_table[z][:].bitcast(U32)
             nc.vector.tensor_copy(x_codes[z][:, first:last], window.indirect(entries(offs_sb, first, last)))
 
-        def turn(source, name):
-            bank = psum.tile([P, S], F32, name=name)
+        def turn(source, name, slot):
+            bank = psum.tile([P, S], F32, name=name, tag=slot)
             for c in range(S // P):
                 block = slice(c * P, (c + 1) * P)
                 nc.tensor.transpose(bank[:, block], source[:, block], identity[:])
@@ -120,31 +117,34 @@ def tile_picked_sinkcol_none_p_kernel(tc, x_words, x_scales, w1, cs, offs, col, 
             nc.vector.tensor_copy(
                 cs_picked[:, first : first + HALF], cs_table[:].indirect(entries(col_sb, first, first + HALF))
             )
-        turned = turn(cs_picked, "turned")
-        w_quant = [quantize_pass(0)]
+        turned = turn(cs_picked, "turned", "scores3_0")
+        by_scalar = regroup(nc.scalar.copy, w_first[:, :, 0 : N // 2], 0, 2, "grouped00")
+        second = quantize(regroup(nc.vector.tensor_copy, w_first[:, :, N // 2 : N], 0, 2, "grouped01"), 2 * P, "w01")
+        w_quant = [quantize(by_scalar, 2 * P, "w00") + second]
 
-        spread = tile([P, S], F32, "spread")
-        one_each = turned[:].rearrange("p (c r) -> p c r", r=STRIPE)[:, :, CS_ROW : CS_ROW + 1]
-        nc.scalar.copy(
-            out=spread[:].rearrange("p (c r) -> p c r", r=STRIPE), in_=one_each.to_broadcast([P, S // STRIPE, STRIPE])
-        )
-        factors = turn(spread, "factors")
+        factors = []
+        for h in range(2):
+            spread = tile([P, S], F32, f"spread{h}")
+            one_each = turned[:].rearrange("p (c h g r) -> p h c g r", h=2, g=4, r=STRIPE)[:, h, :, :, CS_ROW : CS_ROW + 1]
+            nc.scalar.copy(
+                out=spread[:].rearrange("p (c g r) -> p c g r", g=4, r=32), in_=one_each.to_broadcast([P, 4, 4, 32])
+            )
+            factors.append(turn(spread, f"factors{h}", f"factors{h}"))
 
         x_codes = [tile([P, S], U32, f"x_codes{z}") for z in range(PASSES)]
         pick_words(0, 0, S)
         x_planes = tile([P, S], U8, "x_planes")
         nc.vector.tensor_copy(x_planes[:], scale_table[:].indirect(offs_sb[:]))
-        w_quant.append(quantize_pass(1))
+        w_quant.append(quantize(regroup(nc.scalar.copy, w_second[0][:], 0, 2, "grouped10"), 2 * P, "w10"))
         pick_words(1, 0, HALF)
         pick_words(1, HALF, S)
 
         def multiply(bank, t, z, first, last):
-            codes, plane = w_quant[z][t // 2]
-            queries = slice(t % 2 * P, (t % 2 + 1) * P)
+            codes, plane = w_quant[z][t]
             nc.tensor.matmul_mx(
                 out=bank[:],
-                lhsT=codes[:, queries].bitcast(FP8X4),
-                lhsT_scale=plane[:, queries],
+                lhsT=codes.bitcast(FP8X4),
+                lhsT_scale=plane,
                 rhs=x_codes[z][:, first:last].bitcast(FP8X4),
                 rhs_scale=x_planes[SCALE_ROWS * z : P, first:last],
                 start=(z == 0),
@@ -153,10 +153,13 @@ def tile_picked_sinkcol_none_p_kernel(tc, x_words, x_scales, w1, cs, offs, col, 
 
         halves = [(t, first, first + HALF) for first in (0, HALF) for t in range(SPLIT_TILES)]
         pieces = halves + [(t, 0, S) for t in range(SPLIT_TILES, TILES)]
-        scores = {(t, first): psum.tile([P, last - first], F32, name=f"scores{t}_{first}") for t, first, last in pieces}
-        for z in range(PASSES):
-            for t, first, last in pieces:
-                multiply(scores[t, first], t, z, first, last)
+        scores = {(t, first): psum.tile([P, last - first], F32, name=f"scores{t}_{first}", tag=f"scores{t}_{first}") for t, first, last in pieces}
+        for t, first, last in pieces[:-1]:
+            multiply(scores[t, first], t, 0, first, last)
+        for t, first, last in halves:
+            multiply(scores[t, first], t, 1, first, last)
+        multiply(scores[3, 0], 3, 0, 0, S)
+        late = [regroup(nc.scalar.copy, w_second[1][:], u, u + 1, f"late{u}") for u in range(2)]
 
         totals = tile([P, TILES], F32, "totals")
         expd = [tile([P, S], F32, f"expd{t}") for t in range(TILES)]
@@ -173,6 +176,9 @@ def tile_picked_sinkcol_none_p_kernel(tc, x_words, x_scales, w1, cs, offs, col, 
                 op1=ALU.min,
                 accum_out=least[t, first][:],
             )
+        for u in range(2):
+            w_quant[1].extend(quantize(late[u], P, f"w1{2 + u}"))
+            multiply(scores[2 + u, 0], 2 + u, 1, 0, S)
         for t in range(SPLIT_TILES):
             nc.scalar.activation(
                 out=expd[t][:],
@@ -195,14 +201,14 @@ def tile_picked_sinkcol_none_p_kernel(tc, x_words, x_scales, w1, cs, offs, col, 
             nc.gpsimd.tensor_tensor(out=inv[:], in0=totals[:, t : t + 1], in1=minus_one[:], op=ALU.pow)
             return inv
 
-        out_rows = out.rearrange("(a t i) s -> t a i s", t=TILES, i=RUN)
+        out_rows = out.rearrange("(h a u i) s -> h u a i s", h=2, u=2, i=RUN)
 
         def finish(t, inv):
             result = tile([P, S], F32, f"result{t}")
             nc.vector.scalar_tensor_tensor(
-                out=result[:], in0=expd[t][:], scalar=inv[:], in1=factors[:], op0=ALU.mult, op1=ALU.mult
+                out=result[:], in0=expd[t][:], scalar=inv[:], in1=factors[t // 2][:], op0=ALU.mult, op1=ALU.mult
             )
-            nc.sync.dma_start(out=out_rows[t], in_=result[:])
+            nc.sync.dma_start(out=out_rows[t // 2, t % 2], in_=result[:])
 
         for t in range(SPLIT_TILES, TILES):
             exponentiate(t)

@@ -40,8 +40,8 @@ def tile_picked_sinkcol_none_p_kernel(tc, x_words, x_scales, w1, cs, offs, col, 
         sb = ctx.enter_context(tc.tile_pool(name="sb", bufs=1))
         psum = ctx.enter_context(tc.psum_pool(name="psum", bufs=1))
 
-        def tile(shape, dtype, name):
-            return sb.tile(shape, dtype, name=name, tag=name, align_bytes=64)
+        def tile(shape, dtype, name, slot=None):
+            return sb.tile(shape, dtype, name=name, tag=slot or name, align_bytes=64)
 
         def entries(list_tile, first, last):
             return list_tile[:, first // STRIPE : last // STRIPE]
@@ -88,11 +88,18 @@ def tile_picked_sinkcol_none_p_kernel(tc, x_words, x_scales, w1, cs, offs, col, 
         load_words(1)
         load_w(w_second[1], 1, N // 2, N)
 
-        def regroup(copy, raw, first, last, name):
-            grouped = tile([P, (last - first) * K_PASS], BF16, name)
-            dst = grouped[:].rearrange("p (u a i j) -> p u a i j", u=last - first, i=RUN, j=PACK)
+        def regroup(copies, raw, first, name):
+            count = 2 if len(copies) == 2 or first is None else 1
+            grouped = tile([P, count * K_PASS], BF16, name)
+            dst = grouped[:].rearrange("p (u a i j) -> p u a i j", u=count, i=RUN, j=PACK)
             src = raw.rearrange("p j (a u i) -> p u a i j", u=2, i=RUN)
-            copy(out=dst, in_=src[:, first:last])
+            if len(copies) == 2:
+                for u in range(2):
+                    copies[u](out=dst[:, u : u + 1], in_=src[:, u : u + 1])
+            elif first is None:
+                copies[0](out=dst, in_=src)
+            else:
+                copies[0](out=dst, in_=src[:, first : first + 1])
             return grouped
 
         def quantize(grouped, width, name):
@@ -118,9 +125,9 @@ def tile_picked_sinkcol_none_p_kernel(tc, x_words, x_scales, w1, cs, offs, col, 
                 cs_picked[:, first : first + HALF], cs_table[:].indirect(entries(col_sb, first, first + HALF))
             )
         turned = turn(cs_picked, "turned", "scores3_0")
-        by_scalar = regroup(nc.scalar.copy, w_first[:, :, 0 : N // 2], 0, 2, "grouped00")
-        second = quantize(regroup(nc.vector.tensor_copy, w_first[:, :, N // 2 : N], 0, 2, "grouped01"), 2 * P, "w01")
-        w_quant = [quantize(by_scalar, 2 * P, "w00") + second]
+        by_scalar = regroup([nc.scalar.copy], w_first[:, :, 0 : N // 2], None, "grouped00")
+        shared = regroup([nc.scalar.copy, nc.vector.tensor_copy], w_first[:, :, N // 2 : N], None, "grouped01")
+        w_quant = [quantize(by_scalar, 2 * P, "w00") + quantize(shared, 2 * P, "w01")]
 
         factors = []
         for h in range(2):
@@ -135,7 +142,7 @@ def tile_picked_sinkcol_none_p_kernel(tc, x_words, x_scales, w1, cs, offs, col, 
         pick_words(0, 0, S)
         x_planes = tile([P, S], U8, "x_planes")
         nc.vector.tensor_copy(x_planes[:], scale_table[:].indirect(offs_sb[:]))
-        w_quant.append(quantize(regroup(nc.scalar.copy, w_second[0][:], 0, 2, "grouped10"), 2 * P, "w10"))
+        w_quant.append(quantize(regroup([nc.scalar.copy], w_second[0][:], None, "grouped10"), 2 * P, "w10"))
         pick_words(1, 0, HALF)
         pick_words(1, HALF, S)
 
@@ -159,14 +166,15 @@ def tile_picked_sinkcol_none_p_kernel(tc, x_words, x_scales, w1, cs, offs, col, 
         for t, first, last in halves:
             multiply(scores[t, first], t, 1, first, last)
         multiply(scores[3, 0], 3, 0, 0, S)
-        late = [regroup(nc.scalar.copy, w_second[1][:], u, u + 1, f"late{u}") for u in range(2)]
+        late = [regroup([nc.scalar.copy], w_second[1][:], u, f"late{u}") for u in range(2)]
 
         totals = tile([P, TILES], F32, "totals")
         expd = [tile([P, S], F32, f"expd{t}") for t in range(TILES)]
         negated = [tile([P, S], F32, f"negated{t}") for t in range(SPLIT_TILES)]
         least = {}
-        for t, first, last in halves:
-            least[t, first] = tile([P, 1], F32, f"least{t}_{first}")
+
+        def negate(t, first, last, slot=None):
+            least[t, first] = tile([P, 1], F32, f"least{t}_{first}", slot)
             nc.vector.tensor_scalar(
                 out=negated[t][:, first:last],
                 in0=scores[t, first][:],
@@ -176,9 +184,13 @@ def tile_picked_sinkcol_none_p_kernel(tc, x_words, x_scales, w1, cs, offs, col, 
                 op1=ALU.min,
                 accum_out=least[t, first][:],
             )
+
+        for piece in halves[:-1]:
+            negate(*piece)
         for u in range(2):
             w_quant[1].extend(quantize(late[u], P, f"w1{2 + u}"))
             multiply(scores[2 + u, 0], 2 + u, 1, 0, S)
+        negate(*halves[-1], "w_second1")
         for t in range(SPLIT_TILES):
             nc.scalar.activation(
                 out=expd[t][:],

@@ -49,15 +49,19 @@ def tile_picked_sinkcol_none_p_kernel(tc, x_words, x_scales, w1, cs, offs, col, 
         offs_sb = lists.tile([P, S // STRIPE], U16, name="offs_sb")
         col_sb = lists.tile([P, S // STRIPE], U16, name="col_sb")
         scale_table = tile([P, T], U8, "scale_table")
-        word_table = [tile([P, T], I32, f"word_table{z}") for z in range(PASSES)]
+        word_table = {}
+        x_planes = [tile([P, S], U8, f"x_plane{z}") for z in range(PASSES)]
         w_first = tile([P, PACK, N], F32, "w_first")
-        w_second = [tile([P, PACK, N // 2], F32, f"w_second{h}") for h in range(2)]
+        w_second = {}
         cs_table = tile([P, U], F32, "cs_table")
         identity = tile([P, P], F32, "identity")
 
         nc.gpsimd.memset(cs_table[:, 0 : U // 2], 0.0)
         nc.vector.memset(cs_table[:, U // 2 : U], 0.0)
-        nc.vector.memset(scale_table[:].bitcast(I32), 0)
+        nc.vector.memset(scale_table[32:64, :].bitcast(I32), 0)
+        nc.vector.memset(scale_table[64:P, :].bitcast(I32), 0)
+        for plane in x_planes:
+            nc.gpsimd.memset(plane[:].bitcast(I32), 0)
         make_identity(nc, identity[:])
         minus_one = tile([P, 1], F32, "minus_one")
         nc.gpsimd.memset(minus_one[:], -1.0)
@@ -66,27 +70,34 @@ def tile_picked_sinkcol_none_p_kernel(tc, x_words, x_scales, w1, cs, offs, col, 
             rows = w1[z * K_PASS : (z + 1) * K_PASS, first:last]
             nc.sync.dma_start(out=raw[:], in_=rows.rearrange("(p j) n -> p j n", j=PACK))
 
-        def load_scales(rows):
-            for a, z in rows:
-                nc.sync.dma_start(
-                    out=scale_table[SCALE_ROWS * z + a : P : QUADRANT, :].bitcast(I32),
-                    in_=x_scales[z, a :: SCALE_ROWS, :].bitcast(I32),
-                )
-
-        def load_words(z):
+        def load_words(z, slot=None):
+            word_table[z] = tile([P, T], I32, f"word_table{z}", slot)
             nc.sync.dma_start(out=word_table[z][:], in_=x_words[z].rearrange("p c r -> p (c r)").bitcast(I32))
 
-        scale_rows = [(a, z) for a in range(SCALE_ROWS) for z in range(PASSES)]
+        def load_side(h, slot=None):
+            w_second[h] = tile([P, PACK, N // 2], F32, f"w_second{h}", slot)
+            load_w(w_second[h], 1, h * N // 2, (h + 1) * N // 2)
+
+        picked_scales = tile([P, S], U8, "picked_scales")
+
+        def place_scales(z):
+            for a in range(SCALE_ROWS):
+                nc.sync.dma_start(
+                    out=x_planes[z][SCALE_ROWS * z + a : P : QUADRANT, :].bitcast(I32),
+                    in_=picked_scales[16 * z + a : 16 * (z + 1) : SCALE_ROWS, :].bitcast(I32),
+                )
+
+        nc.sync.dma_start(out=scale_table[0:32, :].bitcast(I32), in_=x_scales.rearrange("z q c -> (z q) c").bitcast(I32))
+        nc.sync.dma_start(offs_sb[:], offs)
         load_w(w_first, 0, 0, N)
         nc.sync.dma_start(col_sb[:], col)
-        nc.sync.dma_start(offs_sb[:], offs)
         nc.sync.dma_start(out=cs_table[CS_ROW:P:STRIPE, :], in_=cs[0:N:GROUP, :])
-        load_scales(scale_rows[:SCALES_AHEAD])
         load_words(0)
-        load_scales(scale_rows[SCALES_AHEAD:])
-        load_w(w_second[0], 1, 0, N // 2)
-        load_words(1)
-        load_w(w_second[1], 1, N // 2, N)
+        load_side(0)
+        nc.vector.tensor_copy(picked_scales[:], scale_table[:].indirect(offs_sb[:]))
+        place_scales(0)
+        load_words(1, "scale_table")
+        place_scales(1)
 
         def regroup(copies, raw, first, name):
             count = 2 if len(copies) == 2 or first is None else 1
@@ -124,6 +135,7 @@ def tile_picked_sinkcol_none_p_kernel(tc, x_words, x_scales, w1, cs, offs, col, 
             nc.vector.tensor_copy(
                 cs_picked[:, first : first + HALF], cs_table[:].indirect(entries(col_sb, first, first + HALF))
             )
+        load_side(1, "cs_table")
         turned = turn(cs_picked, "turned", "scores3_0")
         by_scalar = regroup([nc.scalar.copy], w_first[:, :, 0 : N // 2], None, "grouped00")
         shared = regroup([nc.scalar.copy, nc.vector.tensor_copy], w_first[:, :, N // 2 : N], None, "grouped01")
@@ -140,8 +152,6 @@ def tile_picked_sinkcol_none_p_kernel(tc, x_words, x_scales, w1, cs, offs, col, 
 
         x_codes = [tile([P, S], U32, f"x_codes{z}") for z in range(PASSES)]
         pick_words(0, 0, S)
-        x_planes = tile([P, S], U8, "x_planes")
-        nc.vector.tensor_copy(x_planes[:], scale_table[:].indirect(offs_sb[:]))
         w_quant.append(quantize(regroup([nc.scalar.copy], w_second[0][:], None, "grouped10"), 2 * P, "w10"))
         pick_words(1, 0, HALF)
         pick_words(1, HALF, S)
@@ -153,7 +163,7 @@ def tile_picked_sinkcol_none_p_kernel(tc, x_words, x_scales, w1, cs, offs, col, 
                 lhsT=codes.bitcast(FP8X4),
                 lhsT_scale=plane,
                 rhs=x_codes[z][:, first:last].bitcast(FP8X4),
-                rhs_scale=x_planes[SCALE_ROWS * z : P, first:last],
+                rhs_scale=x_planes[z][SCALE_ROWS * z : P, first:last],
                 start=(z == 0),
                 stop=(z == PASSES - 1),
             )
@@ -190,7 +200,7 @@ def tile_picked_sinkcol_none_p_kernel(tc, x_words, x_scales, w1, cs, offs, col, 
         for u in range(2):
             w_quant[1].extend(quantize(late[u], P, f"w1{2 + u}"))
             multiply(scores[2 + u, 0], 2 + u, 1, 0, S)
-        negate(*halves[-1], "w_second1")
+        negate(*halves[-1], "cs_table")
         for t in range(SPLIT_TILES):
             nc.scalar.activation(
                 out=expd[t][:],

@@ -22,15 +22,12 @@ PACK = 4
 K_PASS = P * PACK
 PASSES = K // K_PASS
 TILES = N // P
-SPLIT_TILES = 2
 STRIPE = 16
 HALF = S // 2
 GROUP = 64
-RUN = 8
 QUADRANT = 32
 SCALE_ROWS = 4
 CS_ROW = 8
-SCALES_AHEAD = 3
 
 
 def tile_picked_sinkcol_none_p_kernel(tc, x_words, x_scales, w1, cs, offs, col, out):
@@ -50,9 +47,7 @@ def tile_picked_sinkcol_none_p_kernel(tc, x_words, x_scales, w1, cs, offs, col, 
         col_sb = lists.tile([P, S // STRIPE], U16, name="col_sb")
         scale_table = tile([P, T], U8, "scale_table")
         word_table = {}
-        x_planes = [tile([P, S], U8, f"x_plane{z}") for z in range(PASSES)]
-        w_first = tile([P, PACK, N], F32, "w_first")
-        w_second = {}
+        x_plane = tile([P, PASSES * S], U8, "x_plane")
         cs_table = tile([P, U], F32, "cs_table")
         identity = tile([P, P], F32, "identity")
 
@@ -60,58 +55,45 @@ def tile_picked_sinkcol_none_p_kernel(tc, x_words, x_scales, w1, cs, offs, col, 
         nc.vector.memset(cs_table[:, U // 2 : U], 0.0)
         nc.vector.memset(scale_table[32:64, :].bitcast(I32), 0)
         nc.vector.memset(scale_table[64:P, :].bitcast(I32), 0)
-        for plane in x_planes:
-            nc.gpsimd.memset(plane[:].bitcast(I32), 0)
+        nc.gpsimd.memset(x_plane[:].bitcast(I32), 0)
         make_identity(nc, identity[:])
         minus_one = tile([P, 1], F32, "minus_one")
         nc.gpsimd.memset(minus_one[:], -1.0)
 
-        def load_w(raw, z, first, last):
-            rows = w1[z * K_PASS : (z + 1) * K_PASS, first:last]
+        def load_w(z, first, count, slot=None):
+            raw = tile([P, PACK, count * P], F32, f"w_raw{z}_{first}", slot)
+            rows = w1[z * K_PASS : (z + 1) * K_PASS, first * P : (first + count) * P]
             nc.sync.dma_start(out=raw[:], in_=rows.rearrange("(p j) n -> p j n", j=PACK))
+            return raw
 
         def load_words(z, slot=None):
             word_table[z] = tile([P, T], I32, f"word_table{z}", slot)
             nc.sync.dma_start(out=word_table[z][:], in_=x_words[z].rearrange("p c r -> p (c r)").bitcast(I32))
 
-        def load_side(h, slot=None):
-            w_second[h] = tile([P, PACK, N // 2], F32, f"w_second{h}", slot)
-            load_w(w_second[h], 1, h * N // 2, (h + 1) * N // 2)
-
-        picked_scales = tile([P, S], U8, "picked_scales")
-
-        def place_scales(z):
-            for a in range(SCALE_ROWS):
-                nc.sync.dma_start(
-                    out=x_planes[z][SCALE_ROWS * z + a : P : QUADRANT, :].bitcast(I32),
-                    in_=picked_scales[16 * z + a : 16 * (z + 1) : SCALE_ROWS, :].bitcast(I32),
-                )
-
-        nc.sync.dma_start(out=scale_table[0:32, :].bitcast(I32), in_=x_scales.rearrange("z q c -> (z q) c").bitcast(I32))
+        nc.sync.dma_start(out=scale_table[0:32, :].bitcast(I32), in_=x_scales.rearrange("z q c -> q z c").bitcast(I32))
         nc.sync.dma_start(offs_sb[:], offs)
-        load_w(w_first, 0, 0, N)
+        raw00 = load_w(0, 0, 2)
         nc.sync.dma_start(col_sb[:], col)
         nc.sync.dma_start(out=cs_table[CS_ROW:P:STRIPE, :], in_=cs[0:N:GROUP, :])
+        raw10 = load_w(1, 0, 1)
         load_words(0)
-        load_side(0)
-        nc.vector.tensor_copy(picked_scales[:], scale_table[:].indirect(offs_sb[:]))
-        place_scales(0)
-        load_words(1, "scale_table")
-        place_scales(1)
 
-        def regroup(copies, raw, first, name):
-            count = 2 if len(copies) == 2 or first is None else 1
-            grouped = tile([P, count * K_PASS], BF16, name)
-            dst = grouped[:].rearrange("p (u a i j) -> p u a i j", u=count, i=RUN, j=PACK)
-            src = raw.rearrange("p j (a u i) -> p u a i j", u=2, i=RUN)
-            if len(copies) == 2:
-                for u in range(2):
-                    copies[u](out=dst[:, u : u + 1], in_=src[:, u : u + 1])
-            elif first is None:
-                copies[0](out=dst, in_=src)
-            else:
-                copies[0](out=dst, in_=src[:, first : first + 1])
-            return grouped
+        picked_scales = tile([P, S], U8, "picked_scales")
+        nc.vector.tensor_copy(picked_scales[:], scale_table[:].indirect(offs_sb[:]))
+        rows_each = PASSES * SCALE_ROWS
+        for q in range(P // QUADRANT):
+            nc.sync.dma_start(
+                out=x_plane[QUADRANT * q : QUADRANT * q + SCALE_ROWS, :].bitcast(I32),
+                in_=picked_scales[rows_each * q : rows_each * (q + 1), :].bitcast(I32),
+            )
+        load_words(1, "scale_table")
+
+        def by_pool(out, in_):
+            nc.gpsimd.tensor_scalar(out=out, in0=in_, scalar1=1.0, scalar2=0.0, op0=ALU.mult, op1=ALU.add)
+
+        def regroup(copy, grouped, place, raw, first, last):
+            dst = grouped[:, place * PACK : (place + last - first) * PACK].rearrange("p (n j) -> p n j", j=PACK)
+            copy(out=dst, in_=raw[:, :, first:last].rearrange("p j n -> p n j"))
 
         def quantize(grouped, width, name):
             codes = tile([P, width], U32, f"{name}_codes")
@@ -135,104 +117,109 @@ def tile_picked_sinkcol_none_p_kernel(tc, x_words, x_scales, w1, cs, offs, col, 
             nc.vector.tensor_copy(
                 cs_picked[:, first : first + HALF], cs_table[:].indirect(entries(col_sb, first, first + HALF))
             )
-        load_side(1, "cs_table")
-        turned = turn(cs_picked, "turned", "scores3_0")
-        by_scalar = regroup([nc.scalar.copy], w_first[:, :, 0 : N // 2], None, "grouped00")
-        shared = regroup([nc.scalar.copy, nc.vector.tensor_copy], w_first[:, :, N // 2 : N], None, "grouped01")
-        w_quant = [quantize(by_scalar, 2 * P, "w00") + quantize(shared, 2 * P, "w01")]
+        raw11 = load_w(1, 1, 1, "cs_table")
+        turned = turn(cs_picked, "turned", "scores2")
+        raw02 = load_w(0, 2, 2, "cs_picked")
 
-        factors = []
-        for h in range(2):
-            spread = tile([P, S], F32, f"spread{h}")
-            one_each = turned[:].rearrange("p (c h g r) -> p h c g r", h=2, g=4, r=STRIPE)[:, h, :, :, CS_ROW : CS_ROW + 1]
+        grouped0 = tile([P, 2 * K_PASS], BF16, "grouped0")
+        regroup(nc.scalar.copy, grouped0, 0, raw00, 0, 2 * P)
+        early = tile([P, K_PASS], BF16, "early")
+        regroup(nc.vector.tensor_copy, early, 0, raw10, 0, P)
+        w_quant = {}
+        w_quant[0, 0], w_quant[0, 1] = quantize(grouped0, 2 * P, "w0")
+        (w_quant[1, 0],) = quantize(early, P, "w10")
+
+        factors = {}
+        spreads = []
+        for t in range(TILES):
+            spread = tile([P, S], F32, f"spread{t}")
+            one_each = turned[:].rearrange("p (c t g r) -> p t c g r", t=TILES, g=2, r=STRIPE)[:, t, :, :, CS_ROW : CS_ROW + 1]
             nc.scalar.copy(
-                out=spread[:].rearrange("p (c g r) -> p c g r", g=4, r=32), in_=one_each.to_broadcast([P, 4, 4, 32])
+                out=spread[:].rearrange("p (c g r) -> p c g r", g=2, r=GROUP), in_=one_each.to_broadcast([P, 4, 2, GROUP])
             )
-            factors.append(turn(spread, f"factors{h}", f"factors{h}"))
+            spreads.append(spread)
+            if t < 2:
+                factors[t] = turn(spread, f"factors{t}", f"factors{t}")
+        raw12 = load_w(1, 2, 1, "spread0")
+        raw13 = load_w(1, 3, 1, "spread1")
 
         x_codes = [tile([P, S], U32, f"x_codes{z}") for z in range(PASSES)]
-        pick_words(0, 0, S)
-        w_quant.append(quantize(regroup([nc.scalar.copy], w_second[0][:], None, "grouped10"), 2 * P, "w10"))
-        pick_words(1, 0, HALF)
-        pick_words(1, HALF, S)
+        scores = [psum.tile([P, S], F32, name=f"scores{t}", tag=f"scores{t}") for t in range(TILES)]
 
-        def multiply(bank, t, z, first, last):
-            codes, plane = w_quant[z][t]
+        def multiply(t, z, first, last):
+            codes, plane = w_quant[z, t]
             nc.tensor.matmul_mx(
-                out=bank[:],
+                out=scores[t][:, first:last],
                 lhsT=codes.bitcast(FP8X4),
                 lhsT_scale=plane,
                 rhs=x_codes[z][:, first:last].bitcast(FP8X4),
-                rhs_scale=x_planes[z][SCALE_ROWS * z : P, first:last],
+                rhs_scale=x_plane[:, z * S + first : z * S + last],
                 start=(z == 0),
-                stop=(z == PASSES - 1),
+                stop=(z == PASSES - 1 and last == S),
             )
-
-        halves = [(t, first, first + HALF) for first in (0, HALF) for t in range(SPLIT_TILES)]
-        pieces = halves + [(t, 0, S) for t in range(SPLIT_TILES, TILES)]
-        scores = {(t, first): psum.tile([P, last - first], F32, name=f"scores{t}_{first}", tag=f"scores{t}_{first}") for t, first, last in pieces}
-        for t, first, last in pieces[:-1]:
-            multiply(scores[t, first], t, 0, first, last)
-        for t, first, last in halves:
-            multiply(scores[t, first], t, 1, first, last)
-        multiply(scores[3, 0], 3, 0, 0, S)
-        late = [regroup([nc.scalar.copy], w_second[1][:], u, f"late{u}") for u in range(2)]
 
         totals = tile([P, TILES], F32, "totals")
+        total = [raw13[:, 1, 0:1]] + [totals[:, t : t + 1] for t in range(1, TILES)]
         expd = [tile([P, S], F32, f"expd{t}") for t in range(TILES)]
-        negated = [tile([P, S], F32, f"negated{t}") for t in range(SPLIT_TILES)]
-        least = {}
+        inv = {}
 
-        def negate(t, first, last, slot=None):
-            least[t, first] = tile([P, 1], F32, f"least{t}_{first}", slot)
-            nc.vector.tensor_scalar(
-                out=negated[t][:, first:last],
-                in0=scores[t, first][:],
-                scalar1=-1.0,
-                scalar2=None if first == 0 else least[t, 0][:],
-                op0=ALU.mult,
-                op1=ALU.min,
-                accum_out=least[t, first][:],
-            )
-
-        for piece in halves[:-1]:
-            negate(*piece)
-        for u in range(2):
-            w_quant[1].extend(quantize(late[u], P, f"w1{2 + u}"))
-            multiply(scores[2 + u, 0], 2 + u, 1, 0, S)
-        negate(*halves[-1], "cs_table")
-        for t in range(SPLIT_TILES):
-            nc.scalar.activation(
-                out=expd[t][:],
-                in_=negated[t][:],
-                func=ACT.Exp,
-                scale=-1.0,
-                bias=least[t, HALF][:],
-                accum_out=totals[:, t : t + 1],
-            )
+        maxima = tile([P, TILES], F32, "maxima")
+        neg_max = [raw11[:, 0, 0:1], raw13[:, 0, P - 1 : P], maxima[:, 2:3], maxima[:, 3:4]]
 
         def exponentiate(t):
-            neg_max = tile([P, 1], F32, f"neg_max{t}")
-            nc.vector.tensor_reduce(out=neg_max[:], in_=scores[t, 0][:], axis=AX.X, op=ALU.max, negate=True)
+            nc.vector.tensor_reduce(out=neg_max[t], in_=scores[t][:], axis=AX.X, op=ALU.max, negate=True)
             nc.scalar.activation(
-                out=expd[t][:], in_=scores[t, 0][:], func=ACT.Exp, bias=neg_max[:], accum_out=totals[:, t : t + 1]
+                out=expd[t][:], in_=scores[t][:], func=ACT.Exp, bias=neg_max[t], accum_out=total[t]
             )
 
         def invert(t):
-            inv = tile([P, 1], F32, f"inv{t}")
-            nc.gpsimd.tensor_tensor(out=inv[:], in0=totals[:, t : t + 1], in1=minus_one[:], op=ALU.pow)
-            return inv
+            power = tile([P, 1], F32, f"inv{t}")
+            inv[t] = power[:]
+            nc.gpsimd.tensor_tensor(out=inv[t], in0=total[t], in1=minus_one[:], op=ALU.pow)
 
-        out_rows = out.rearrange("(h a u i) s -> h u a i s", h=2, u=2, i=RUN)
-
-        def finish(t, inv):
-            result = tile([P, S], F32, f"result{t}")
+        def finish(t, slot=None):
+            result = tile([P, S], F32, f"result{t}", slot)
             nc.vector.scalar_tensor_tensor(
-                out=result[:], in0=expd[t][:], scalar=inv[:], in1=factors[t // 2][:], op0=ALU.mult, op1=ALU.mult
+                out=result[:], in0=expd[t][:], scalar=inv[t], in1=factors[t][:], op0=ALU.mult, op1=ALU.mult
             )
-            nc.sync.dma_start(out=out_rows[t // 2, t % 2], in_=result[:])
+            nc.sync.dma_start(out=out[t * P : (t + 1) * P, :], in_=result[:])
 
-        for t in range(SPLIT_TILES, TILES):
-            exponentiate(t)
-        for t in range(TILES):
-            finish(t, invert(t))
+        pick_words(0, 0, S)
+        multiply(0, 0, 0, S)
+        multiply(1, 0, 0, S)
+        for first in (0, HALF):
+            pick_words(1, first, first + HALF)
+            multiply(0, 1, first, first + HALF)
+
+        late1 = tile([P, K_PASS], BF16, "late1")
+        regroup(nc.scalar.copy, late1, 0, raw11, 0, P)
+        (w_quant[1, 1],) = quantize(late1, P, "w11")
+        multiply(1, 1, 0, S)
+
+        grouped2 = tile([P, 2 * K_PASS], BF16, "grouped2")
+        regroup(nc.scalar.copy, grouped2, 0, raw02, 0, P)
+        regroup(by_pool, grouped2, P, raw02, P, 2 * P)
+        w_quant[0, 2], w_quant[0, 3] = quantize(grouped2, 2 * P, "w2")
+        multiply(2, 0, 0, S)
+        multiply(3, 0, 0, S)
+
+        late2 = tile([P, K_PASS], BF16, "late2")
+        regroup(nc.scalar.copy, late2, 0, raw12, 0, P)
+        late3 = tile([P, K_PASS], BF16, "late3")
+        regroup(by_pool, late3, 0, raw13, 0, P // 4)
+        regroup(nc.scalar.copy, late3, P // 4, raw13, P // 4, P)
+        exponentiate(0)
+        (w_quant[1, 2],) = quantize(late2, P, "w12")
+        multiply(2, 1, 0, S)
+        (w_quant[1, 3],) = quantize(late3, P, "w13")
+        multiply(3, 1, 0, S)
+        exponentiate(1)
+        exponentiate(2)
+        exponentiate(3)
+        invert(0)
+        finish(0, "w13_codes")
+        factors[2] = turn(spreads[2], "factors2", "scores1")
+        factors[3] = turn(spreads[3], "factors3", "factors0")
+        for t in range(1, TILES):
+            invert(t)
+            finish(t)

@@ -47,7 +47,7 @@ def tile_picked_sinkcol_none_p_kernel(tc, x_words, x_scales, w1, cs, offs, col, 
         col_sb = lists.tile([P, S // STRIPE], U16, name="col_sb")
         scale_table = tile([P, T], U8, "scale_table")
         word_table = {}
-        x_plane = tile([P, PASSES * S], U8, "x_plane")
+        x_planes = [tile([P, S], U8, f"x_plane{z}") for z in range(PASSES)]
         cs_table = tile([P, U], F32, "cs_table")
         identity = tile([P, P], F32, "identity")
 
@@ -55,7 +55,8 @@ def tile_picked_sinkcol_none_p_kernel(tc, x_words, x_scales, w1, cs, offs, col, 
         nc.vector.memset(cs_table[:, U // 2 : U], 0.0)
         nc.vector.memset(scale_table[32:64, :].bitcast(I32), 0)
         nc.vector.memset(scale_table[64:P, :].bitcast(I32), 0)
-        nc.gpsimd.memset(x_plane[:].bitcast(I32), 0)
+        for plane in x_planes:
+            nc.gpsimd.memset(plane[:].bitcast(I32), 0)
         make_identity(nc, identity[:])
         minus_one = tile([P, 1], F32, "minus_one")
         nc.gpsimd.memset(minus_one[:], -1.0)
@@ -70,7 +71,7 @@ def tile_picked_sinkcol_none_p_kernel(tc, x_words, x_scales, w1, cs, offs, col, 
             word_table[z] = tile([P, T], I32, f"word_table{z}", slot)
             nc.sync.dma_start(out=word_table[z][:], in_=x_words[z].rearrange("p c r -> p (c r)").bitcast(I32))
 
-        nc.sync.dma_start(out=scale_table[0:32, :].bitcast(I32), in_=x_scales.rearrange("z q c -> q z c").bitcast(I32))
+        nc.sync.dma_start(out=scale_table[0:32, :].bitcast(I32), in_=x_scales.rearrange("z q c -> (z q) c").bitcast(I32))
         nc.sync.dma_start(offs_sb[:], offs)
         raw00 = load_w(0, 0, 2)
         nc.sync.dma_start(col_sb[:], col)
@@ -80,13 +81,17 @@ def tile_picked_sinkcol_none_p_kernel(tc, x_words, x_scales, w1, cs, offs, col, 
 
         picked_scales = tile([P, S], U8, "picked_scales")
         nc.vector.tensor_copy(picked_scales[:], scale_table[:].indirect(offs_sb[:]))
-        rows_each = PASSES * SCALE_ROWS
-        for q in range(P // QUADRANT):
-            nc.sync.dma_start(
-                out=x_plane[QUADRANT * q : QUADRANT * q + SCALE_ROWS, :].bitcast(I32),
-                in_=picked_scales[rows_each * q : rows_each * (q + 1), :].bitcast(I32),
-            )
+
+        def place_scales(z):
+            for a in range(SCALE_ROWS):
+                nc.sync.dma_start(
+                    out=x_planes[z][SCALE_ROWS * z + a : P : QUADRANT, :].bitcast(I32),
+                    in_=picked_scales[16 * z + a : 16 * (z + 1) : SCALE_ROWS, :].bitcast(I32),
+                )
+
+        place_scales(0)
         load_words(1, "scale_table")
+        place_scales(1)
 
         def by_pool(out, in_):
             nc.gpsimd.tensor_scalar(out=out, in0=in_, scalar1=1.0, scalar2=0.0, op0=ALU.mult, op1=ALU.add)
@@ -153,13 +158,13 @@ def tile_picked_sinkcol_none_p_kernel(tc, x_words, x_scales, w1, cs, offs, col, 
                 lhsT=codes.bitcast(FP8X4),
                 lhsT_scale=plane,
                 rhs=x_codes[z][:, first:last].bitcast(FP8X4),
-                rhs_scale=x_plane[:, z * S + first : z * S + last],
+                rhs_scale=x_planes[z][SCALE_ROWS * z : P, first:last],
                 start=(z == 0),
                 stop=(z == PASSES - 1 and last == S),
             )
 
         totals = tile([P, TILES], F32, "totals")
-        total = [raw13[:, 1, 0:1]] + [totals[:, t : t + 1] for t in range(1, TILES)]
+        total = [raw13[:, 0, 0:1]] + [totals[:, t : t + 1] for t in range(1, TILES)]
         expd = [tile([P, S], F32, f"expd{t}") for t in range(TILES)]
         inv = {}
 
@@ -206,8 +211,8 @@ def tile_picked_sinkcol_none_p_kernel(tc, x_words, x_scales, w1, cs, offs, col, 
         late2 = tile([P, K_PASS], BF16, "late2")
         regroup(nc.scalar.copy, late2, 0, raw12, 0, P)
         late3 = tile([P, K_PASS], BF16, "late3")
-        regroup(by_pool, late3, 0, raw13, 0, P // 4)
-        regroup(nc.scalar.copy, late3, P // 4, raw13, P // 4, P)
+        for first in (0, P // 2):
+            regroup(nc.scalar.copy, late3, first, raw13, first, first + P // 2)
         exponentiate(0)
         (w_quant[1, 2],) = quantize(late2, P, "w12")
         multiply(2, 1, 0, S)

@@ -47,7 +47,7 @@ def tile_picked_sinkcol_none_p_kernel(tc, x_words, x_scales, w1, cs, offs, col, 
         col_sb = lists.tile([P, S // STRIPE], U16, name="col_sb")
         scale_table = tile([P, T], U8, "scale_table")
         word_table = {}
-        x_planes = [tile([P, S], U8, f"x_plane{z}") for z in range(PASSES)]
+        x_plane = tile([P, S], U8, "x_plane")
         cs_table = tile([P, U], F32, "cs_table")
         identity = tile([P, P], F32, "identity")
 
@@ -55,8 +55,7 @@ def tile_picked_sinkcol_none_p_kernel(tc, x_words, x_scales, w1, cs, offs, col, 
         nc.vector.memset(cs_table[:, U // 2 : U], 0.0)
         nc.vector.memset(scale_table[32:64, :].bitcast(I32), 0)
         nc.vector.memset(scale_table[64:P, :].bitcast(I32), 0)
-        for plane in x_planes:
-            nc.gpsimd.memset(plane[:].bitcast(I32), 0)
+        nc.gpsimd.memset(x_plane[:].bitcast(I32), 0)
         make_identity(nc, identity[:])
         minus_one = tile([P, 1], F32, "minus_one")
         nc.gpsimd.memset(minus_one[:], -1.0)
@@ -85,7 +84,7 @@ def tile_picked_sinkcol_none_p_kernel(tc, x_words, x_scales, w1, cs, offs, col, 
         def place_scales(z):
             for a in range(SCALE_ROWS):
                 nc.sync.dma_start(
-                    out=x_planes[z][SCALE_ROWS * z + a : P : QUADRANT, :].bitcast(I32),
+                    out=x_plane[SCALE_ROWS * z + a : P : QUADRANT, :].bitcast(I32),
                     in_=picked_scales[16 * z + a : 16 * (z + 1) : SCALE_ROWS, :].bitcast(I32),
                 )
 
@@ -158,7 +157,7 @@ def tile_picked_sinkcol_none_p_kernel(tc, x_words, x_scales, w1, cs, offs, col, 
                 lhsT=codes.bitcast(FP8X4),
                 lhsT_scale=plane,
                 rhs=x_codes[z][:, first:last].bitcast(FP8X4),
-                rhs_scale=x_planes[z][SCALE_ROWS * z : P, first:last],
+                rhs_scale=x_plane[SCALE_ROWS * z : P, first:last],
                 start=(z == 0),
                 stop=(z == PASSES - 1 and last == S),
             )
@@ -191,10 +190,10 @@ def tile_picked_sinkcol_none_p_kernel(tc, x_words, x_scales, w1, cs, offs, col, 
 
         pick_words(0, 0, S)
         multiply(0, 0, 0, S)
-        multiply(1, 0, 0, S)
         for first in (0, HALF):
             pick_words(1, first, first + HALF)
             multiply(0, 1, first, first + HALF)
+        multiply(1, 0, 0, S)
 
         late1 = tile([P, K_PASS], BF16, "late1")
         regroup(nc.scalar.copy, late1, 0, raw11, 0, P)

@@ -27,6 +27,7 @@ HALF = S // 2
 GROUP = 64
 QUADRANT = 32
 SCALE_ROWS = 4
+LINE = 4
 CS_ROW = 8
 
 
@@ -92,12 +93,12 @@ def tile_picked_sinkcol_none_p_kernel(tc, x_words, x_scales, w1, cs, offs, col, 
         load_words(1, "scale_table")
         place_scales(1)
 
-        def by_pool(out, in_):
-            nc.gpsimd.tensor_scalar(out=out, in0=in_, scalar1=1.0, scalar2=0.0, op0=ALU.mult, op1=ALU.add)
-
         def regroup(copy, grouped, place, raw, first, last):
-            dst = grouped[:, place * PACK : (place + last - first) * PACK].rearrange("p (n j) -> p n j", j=PACK)
-            copy(out=dst, in_=raw[:, :, first:last].rearrange("p j n -> p n j"))
+            dst = grouped[:, place * PACK : (place + last - first) * PACK]
+            copy(
+                out=dst.rearrange("p (c i j) -> p c j i", i=LINE, j=PACK),
+                in_=raw[:, :, first:last].rearrange("p j (c i) -> p c j i", i=LINE),
+            )
 
         def quantize(grouped, width, name):
             codes = tile([P, width], U32, f"{name}_codes")
@@ -163,12 +164,12 @@ def tile_picked_sinkcol_none_p_kernel(tc, x_words, x_scales, w1, cs, offs, col, 
             )
 
         totals = tile([P, TILES], F32, "totals")
-        total = [raw13[:, 0, 0:1]] + [totals[:, t : t + 1] for t in range(1, TILES)]
+        total = [raw13[:, 0, 0:1], raw13[:, 1, 0:1], totals[:, 2:3], totals[:, 3:4]]
         expd = [tile([P, S], F32, f"expd{t}") for t in range(TILES)]
         inv = {}
 
         maxima = tile([P, TILES], F32, "maxima")
-        neg_max = [raw11[:, 0, 0:1], raw13[:, 0, P - 1 : P], maxima[:, 2:3], maxima[:, 3:4]]
+        neg_max = [raw11[:, 0, 0:1], raw12[:, 0, 0:1], maxima[:, 2:3], maxima[:, 3:4]]
 
         def exponentiate(t):
             nc.vector.tensor_reduce(out=neg_max[t], in_=scores[t][:], axis=AX.X, op=ALU.max, negate=True)
@@ -202,7 +203,14 @@ def tile_picked_sinkcol_none_p_kernel(tc, x_words, x_scales, w1, cs, offs, col, 
 
         grouped2 = tile([P, 2 * K_PASS], BF16, "grouped2")
         regroup(nc.scalar.copy, grouped2, 0, raw02, 0, P)
-        regroup(by_pool, grouped2, P, raw02, P, 2 * P)
+        nc.gpsimd.tensor_scalar(
+            out=grouped2[:, K_PASS:].rearrange("p (n j) -> p n j", j=PACK),
+            in0=raw02[:, :, P:].rearrange("p j n -> p n j"),
+            scalar1=1.0,
+            scalar2=0.0,
+            op0=ALU.mult,
+            op1=ALU.add,
+        )
         w_quant[0, 2], w_quant[0, 3] = quantize(grouped2, 2 * P, "w2")
         multiply(2, 0, 0, S)
         multiply(3, 0, 0, S)
@@ -223,7 +231,7 @@ def tile_picked_sinkcol_none_p_kernel(tc, x_words, x_scales, w1, cs, offs, col, 
         invert(0)
         finish(0, "w13_codes")
         factors[2] = turn(spreads[2], "factors2", "scores1")
-        factors[3] = turn(spreads[3], "factors3", "factors0")
+        factors[3] = turn(spreads[3], "factors3", "scores2")
         for t in range(1, TILES):
             invert(t)
             finish(t)

@@ -48,7 +48,7 @@ def tile_picked_sinkcol_none_p_kernel(tc, x_words, x_scales, w1, cs, offs, col, 
         col_sb = lists.tile([P, S // STRIPE], U16, name="col_sb")
         scale_table = tile([P, T], U8, "scale_table")
         word_table = {}
-        x_plane = tile([P, S], U8, "x_plane")
+        x_plane = tile([P, PASSES * S], U8, "x_plane")
         cs_table = tile([P, U], F32, "cs_table")
         identity = tile([P, P], F32, "identity")
 
@@ -71,7 +71,7 @@ def tile_picked_sinkcol_none_p_kernel(tc, x_words, x_scales, w1, cs, offs, col, 
             word_table[z] = tile([P, T], I32, f"word_table{z}", slot)
             nc.sync.dma_start(out=word_table[z][:], in_=x_words[z].rearrange("p c r -> p (c r)").bitcast(I32))
 
-        nc.sync.dma_start(out=scale_table[0:32, :].bitcast(I32), in_=x_scales.rearrange("z q c -> (z q) c").bitcast(I32))
+        nc.sync.dma_start(out=scale_table[0:32, :].bitcast(I32), in_=x_scales.rearrange("z q c -> q z c").bitcast(I32))
         nc.sync.dma_start(offs_sb[:], offs)
         raw00 = load_w(0, 0, 2)
         nc.sync.dma_start(col_sb[:], col)
@@ -81,17 +81,13 @@ def tile_picked_sinkcol_none_p_kernel(tc, x_words, x_scales, w1, cs, offs, col, 
 
         picked_scales = tile([P, S], U8, "picked_scales")
         nc.vector.tensor_copy(picked_scales[:], scale_table[:].indirect(offs_sb[:]))
-
-        def place_scales(z):
-            for a in range(SCALE_ROWS):
-                nc.sync.dma_start(
-                    out=x_plane[SCALE_ROWS * z + a : P : QUADRANT, :].bitcast(I32),
-                    in_=picked_scales[16 * z + a : 16 * (z + 1) : SCALE_ROWS, :].bitcast(I32),
-                )
-
-        place_scales(0)
         load_words(1, "scale_table")
-        place_scales(1)
+        rows_each = PASSES * SCALE_ROWS
+        for q in range(P // QUADRANT):
+            nc.sync.dma_start(
+                out=x_plane[QUADRANT * q : QUADRANT * q + SCALE_ROWS, :].bitcast(I32),
+                in_=picked_scales[rows_each * q : rows_each * (q + 1), :].bitcast(I32),
+            )
 
         def regroup(copy, grouped, place, raw, first, last):
             dst = grouped[:, place * PACK : (place + last - first) * PACK]
@@ -158,7 +154,7 @@ def tile_picked_sinkcol_none_p_kernel(tc, x_words, x_scales, w1, cs, offs, col, 
                 lhsT=codes.bitcast(FP8X4),
                 lhsT_scale=plane,
                 rhs=x_codes[z][:, first:last].bitcast(FP8X4),
-                rhs_scale=x_plane[SCALE_ROWS * z : P, first:last],
+                rhs_scale=x_plane[:, z * S + first : z * S + last],
                 start=(z == 0),
                 stop=(z == PASSES - 1 and last == S),
             )
@@ -182,12 +178,17 @@ def tile_picked_sinkcol_none_p_kernel(tc, x_words, x_scales, w1, cs, offs, col, 
             inv[t] = power[:]
             nc.gpsimd.tensor_tensor(out=inv[t], in0=total[t], in1=minus_one[:], op=ALU.pow)
 
-        def finish(t, slot=None):
-            result = tile([P, S], F32, f"result{t}", slot)
+        def finish(t, first, last, slot=None):
+            result = tile([P, last - first], F32, f"result{t}_{first}", slot)
             nc.vector.scalar_tensor_tensor(
-                out=result[:], in0=expd[t][:], scalar=inv[t], in1=factors[t][:], op0=ALU.mult, op1=ALU.mult
+                out=result[:],
+                in0=expd[t][:, first:last],
+                scalar=inv[t],
+                in1=factors[t][:, first:last],
+                op0=ALU.mult,
+                op1=ALU.mult,
             )
-            nc.sync.dma_start(out=out[t * P : (t + 1) * P, :], in_=result[:])
+            nc.sync.dma_start(out=out[t * P : (t + 1) * P, first:last], in_=result[:])
 
         pick_words(0, 0, S)
         multiply(0, 0, 0, S)
@@ -229,9 +230,13 @@ def tile_picked_sinkcol_none_p_kernel(tc, x_words, x_scales, w1, cs, offs, col, 
         exponentiate(2)
         exponentiate(3)
         invert(0)
-        finish(0, "w13_codes")
+        finish(0, 0, P, "w13_codes")
+        finish(0, P, S, "w13_plane")
         factors[2] = turn(spreads[2], "factors2", "scores1")
         factors[3] = turn(spreads[3], "factors3", "scores2")
         for t in range(1, TILES):
             invert(t)
-            finish(t)
+        finish(1, 0, S)
+        finish(2, 0, S)
+        finish(3, 0, HALF)
+        finish(3, HALF, S)

@@ -165,7 +165,7 @@ def tile_picked_sinkcol_none_p_kernel(tc, x_words, x_scales, w1, cs, offs, col, 
         inv = {}
 
         maxima = tile([P, TILES], F32, "maxima")
-        neg_max = [raw11[:, 0, 0:1], raw12[:, 0, 0:1], maxima[:, 2:3], maxima[:, 3:4]]
+        neg_max = [raw02[:, 0, P : P + 1], raw12[:, 0, 0:1], maxima[:, 2:3], maxima[:, 3:4]]
 
         def exponentiate(t):
             nc.vector.tensor_reduce(out=neg_max[t], in_=scores[t][:], axis=AX.X, op=ALU.max, negate=True)
@@ -204,14 +204,8 @@ def tile_picked_sinkcol_none_p_kernel(tc, x_words, x_scales, w1, cs, offs, col, 
 
         grouped2 = tile([P, 2 * K_PASS], BF16, "grouped2")
         regroup(nc.scalar.copy, grouped2, 0, raw02, 0, P)
-        nc.gpsimd.tensor_scalar(
-            out=grouped2[:, K_PASS:].rearrange("p (n j) -> p n j", j=PACK),
-            in0=raw02[:, :, P:].rearrange("p j n -> p n j"),
-            scalar1=1.0,
-            scalar2=0.0,
-            op0=ALU.mult,
-            op1=ALU.add,
-        )
+        for first in (P, P + P // 2):
+            regroup(nc.vector.tensor_copy, grouped2, first, raw02, first, first + P // 2)
         w_quant[0, 2], w_quant[0, 3] = quantize(grouped2, 2 * P, "w2")
         multiply(2, 0, 0, S)
         multiply(3, 0, 0, S)

from contextlib import ExitStack

import concourse.mybir as mybir
from concourse.masks import make_identity

K, T, S, N, U = 1024, 2048, 512, 512, 512
FLOPS = 2 * K * N * S

F32 = mybir.dt.float32
BF16 = mybir.dt.bfloat16
I32 = mybir.dt.int32
U32 = mybir.dt.uint32
U16 = mybir.dt.uint16
U8 = mybir.dt.uint8
FP8X4 = mybir.dt.float8_e4m3fn_x4
ALU = mybir.AluOpType
ACT = mybir.ActivationFunctionType
AX = mybir.AxisListType

P = 128
PACK = 4
K_PASS = P * PACK
PASSES = K // K_PASS
TILES = N // P
STRIPE = 16
HALF = S // 2
GROUP = 64
QUADRANT = 32
SCALE_ROWS = 4
LINE = 4
CS_ROW = 8


def tile_picked_sinkcol_none_p_kernel(tc, x_words, x_scales, w1, cs, offs, col, out):
    nc = tc.nc
    with ExitStack() as ctx:
        lists = ctx.enter_context(tc.tile_pool(name="lists", bufs=1))
        sb = ctx.enter_context(tc.tile_pool(name="sb", bufs=1))
        psum = ctx.enter_context(tc.psum_pool(name="psum", bufs=1))

        def tile(shape, dtype, name, slot=None):
            return sb.tile(shape, dtype, name=name, tag=slot or name, align_bytes=64)

        def entries(list_tile, first, last):
            return list_tile[:, first // STRIPE : last // STRIPE]

        offs_sb = lists.tile([P, S // STRIPE], U16, name="offs_sb")
        col_sb = lists.tile([P, S // STRIPE], U16, name="col_sb")
        scale_table = tile([P, T], U8, "scale_table")
        word_table = {}
        x_plane = tile([P, PASSES * S], U8, "x_plane")
        cs_table = tile([P, U], F32, "cs_table")
        identity = tile([P, P], F32, "identity")

        nc.gpsimd.memset(cs_table[:, 0 : U // 2], 0.0)
        nc.vector.memset(cs_table[:, U // 2 : U], 0.0)
        nc.vector.memset(scale_table[32:64, :].bitcast(I32), 0)
        nc.vector.memset(scale_table[64:P, :].bitcast(I32), 0)
        nc.gpsimd.memset(x_plane[:].bitcast(I32), 0)
        make_identity(nc, identity[:])
        minus_one = tile([P, 1], F32, "minus_one")
        nc.gpsimd.memset(minus_one[:], -1.0)

        def load_w(z, first, count, slot=None):
            raw = tile([P, PACK, count * P], F32, f"w_raw{z}_{first}", slot)
            rows = w1[z * K_PASS : (z + 1) * K_PASS, first * P : (first + count) * P]
            nc.sync.dma_start(out=raw[:], in_=rows.rearrange("(p j) n -> p j n", j=PACK))
            return raw

        def load_words(z, slot=None):
            word_table[z] = tile([P, T], I32, f"word_table{z}", slot)
            nc.sync.dma_start(out=word_table[z][:], in_=x_words[z].rearrange("p c r -> p (c r)").bitcast(I32))

        nc.sync.dma_start(out=scale_table[0:32, :].bitcast(I32), in_=x_scales.rearrange("z q c -> q z c").bitcast(I32))
        nc.sync.dma_start(offs_sb[:], offs)
        raw00 = load_w(0, 0, 2)
        nc.sync.dma_start(col_sb[:], col)
        nc.sync.dma_start(out=cs_table[CS_ROW:P:STRIPE, :], in_=cs[0:N:GROUP, :])
        raw10 = load_w(1, 0, 1)
        load_words(0)

        picked_scales = tile([P, S], U8, "picked_scales")
        nc.vector.tensor_copy(picked_scales[:], scale_table[:].indirect(offs_sb[:]))
        load_words(1, "scale_table")
        rows_each = PASSES * SCALE_ROWS
        for q in range(P // QUADRANT):
            nc.sync.dma_start(
                out=x_plane[QUADRANT * q : QUADRANT * q + SCALE_ROWS, :].bitcast(I32),
                in_=picked_scales[rows_each * q : rows_each * (q + 1), :].bitcast(I32),
            )

        def regroup(copy, grouped, place, raw, first, last):
            dst = grouped[:, place * PACK : (place + last - first) * PACK]
            copy(
                out=dst.rearrange("p (c i j) -> p c j i", i=LINE, j=PACK),
                in_=raw[:, :, first:last].rearrange("p j (c i) -> p c j i", i=LINE),
            )

        def quantize(grouped, width, name):
            codes = tile([P, width], U32, f"{name}_codes")
            plane = tile([P, width], U8, f"{name}_plane")
            nc.vector.quantize_mx(out=codes[:].bitcast(FP8X4), scales=plane[:], in_=grouped[:])
            return [(codes[:, c : c + P], plane[:, c : c + P]) for c in range(0, width, P)]

        def pick_words(z, first, last):
            window = word_table[z][:].bitcast(U32)
            nc.vector.tensor_copy(x_codes[z][:, first:last], window.indirect(entries(offs_sb, first, last)))

        def turn(source, name, slot):
            bank = psum.tile([P, S], F32, name=name, tag=slot)
            for c in range(S // P):
                block = slice(c * P, (c + 1) * P)
                nc.tensor.transpose(bank[:, block], source[:, block], identity[:])
            return bank

        cs_picked = tile([P, S], F32, "cs_picked")
        for first in (0, HALF):
            nc.vector.tensor_copy(
                cs_picked[:, first : first + HALF], cs_table[:].indirect(entries(col_sb, first, first + HALF))
            )
        raw11 = load_w(1, 1, 1, "cs_table")
        turned = turn(cs_picked, "turned", "scores2")
        raw02 = load_w(0, 2, 2, "cs_picked")

        grouped0 = tile([P, 2 * K_PASS], BF16, "grouped0")
        regroup(nc.scalar.copy, grouped0, 0, raw00, 0, 2 * P)
        early = tile([P, K_PASS], BF16, "early")
        regroup(nc.vector.tensor_copy, early, 0, raw10, 0, P)
        w_quant = {}
        w_quant[0, 0], w_quant[0, 1] = quantize(grouped0, 2 * P, "w0")
        (w_quant[1, 0],) = quantize(early, P, "w10")

        factors = {}
        spreads = []
        for t in range(TILES):
            spread = tile([P, S], F32, f"spread{t}")
            one_each = turned[:].rearrange("p (c t g r) -> p t c g r", t=TILES, g=2, r=STRIPE)[:, t, :, :, CS_ROW : CS_ROW + 1]
            nc.scalar.copy(
                out=spread[:].rearrange("p (c g r) -> p c g r", g=2, r=GROUP), in_=one_each.to_broadcast([P, 4, 2, GROUP])
            )
            spreads.append(spread)
            if t < 2:
                factors[t] = turn(spread, f"factors{t}", f"factors{t}")
        raw12 = load_w(1, 2, 1, "spread0")
        raw13 = load_w(1, 3, 1, "spread1")

        x_codes = [tile([P, S], U32, f"x_codes{z}") for z in range(PASSES)]
        scores = [psum.tile([P, S], F32, name=f"scores{t}", tag=f"scores{t}") for t in range(TILES)]

        def multiply(t, z, first, last):
            codes, plane = w_quant[z, t]
            nc.tensor.matmul_mx(
                out=scores[t][:, first:last],
                lhsT=codes.bitcast(FP8X4),
                lhsT_scale=plane,
                rhs=x_codes[z][:, first:last].bitcast(FP8X4),
                rhs_scale=x_plane[:, z * S + first : z * S + last],
                start=(z == 0),
                stop=(z == PASSES - 1 and last == S),
            )

        totals = tile([P, TILES], F32, "totals")
        total = [raw13[:, 0, 0:1], raw13[:, 1, 0:1], totals[:, 2:3], totals[:, 3:4]]
        expd = [tile([P, S], F32, f"expd{t}") for t in range(TILES)]
        inv = {}

        maxima = tile([P, TILES], F32, "maxima")
        neg_max = [raw02[:, 0, P : P + 1], raw12[:, 0, 0:1], maxima[:, 2:3], maxima[:, 3:4]]

        def exponentiate(t):
            nc.vector.tensor_reduce(out=neg_max[t], in_=scores[t][:], axis=AX.X, op=ALU.max, negate=True)
            nc.scalar.activation(
                out=expd[t][:], in_=scores[t][:], func=ACT.Exp, bias=neg_max[t], accum_out=total[t]
            )

        def invert(t):
            power = tile([P, 1], F32, f"inv{t}")
            inv[t] = power[:]
            nc.gpsimd.tensor_tensor(out=inv[t], in0=total[t], in1=minus_one[:], op=ALU.pow)

        def finish(t, first, last, slot=None):
            result = tile([P, last - first], F32, f"result{t}_{first}", slot)
            nc.vector.scalar_tensor_tensor(
                out=result[:],
                in0=expd[t][:, first:last],
                scalar=inv[t],
                in1=factors[t][:, first:last],
                op0=ALU.mult,
                op1=ALU.mult,
            )
            nc.sync.dma_start(out=out[t * P : (t + 1) * P, first:last], in_=result[:])

        pick_words(0, 0, S)
        multiply(0, 0, 0, S)
        for first in (0, HALF):
            pick_words(1, first, first + HALF)
            multiply(0, 1, first, first + HALF)
        multiply(1, 0, 0, S)

        late1 = tile([P, K_PASS], BF16, "late1")
        regroup(nc.scalar.copy, late1, 0, raw11, 0, P)
        (w_quant[1, 1],) = quantize(late1, P, "w11")
        multiply(1, 1, 0, S)

        grouped2 = tile([P, 2 * K_PASS], BF16, "grouped2")
        regroup(nc.scalar.copy, grouped2, 0, raw02, 0, P)
        for first in (P, P + P // 2):
            regroup(nc.vector.tensor_copy, grouped2, first, raw02, first, first + P // 2)
        w_quant[0, 2], w_quant[0, 3] = quantize(grouped2, 2 * P, "w2")
        multiply(2, 0, 0, S)
        multiply(3, 0, 0, S)

        late2 = tile([P, K_PASS], BF16, "late2")
        regroup(nc.scalar.copy, late2, 0, raw12, 0, P)
        late3 = tile([P, K_PASS], BF16, "late3")
        for first in (0, P // 2):
            regroup(nc.scalar.copy, late3, first, raw13, first, first + P // 2)
        exponentiate(0)
        (w_quant[1, 2],) = quantize(late2, P, "w12")
        multiply(2, 1, 0, S)
        (w_quant[1, 3],) = quantize(late3, P, "w13")
        multiply(3, 1, 0, S)
        exponentiate(1)
        exponentiate(2)
        exponentiate(3)
        invert(0)
        finish(0, 0, P, "w13_codes")
        finish(0, P, S, "w13_plane")
        factors[2] = turn(spreads[2], "factors2", "scores1")
        factors[3] = turn(spreads[3], "factors3", "scores2")
        for t in range(1, TILES):
            invert(t)
        finish(1, 0, S)
        finish(2, 0, S)
        finish(3, 0, HALF)
        finish(3, HALF, S)
